import numpy as np, ml_dtypes
CORES = [16,17,18,19,32,33,34,35]
N = 8
import mx_ref
BF = ml_dtypes.bfloat16
def gentries(a):
    return np.ascontiguousarray(a.reshape(8, 16, -1).transpose(0, 2, 1)).reshape(8, -1)
def gtable(e):
    e = np.asarray(e); return np.ascontiguousarray(e.reshape(8, -1, 16).transpose(0, 2, 1)).reshape(128, -1).astype(np.int32)
def gcols(t, e):
    v = np.concatenate([t.reshape(8, 16, -1, 4), np.zeros((8, 16, 1, 4), BF)], axis=2)
    return np.ascontiguousarray(np.stack([v[g][:, e[g]] for g in range(8)])).reshape(128, -1)
def gpick(z, e):
    return np.concatenate([z[16 * g:16 * g + 16][:, e[g]] for g in range(8)])
def f(rng, *shape):
    return mx_ref.flush((rng.standard_normal(shape, dtype=np.float32) * np.exp2(rng.integers(-2, 3, shape[:-1] + (1,)))).astype(BF))
def wide(rng, *shape, cols=0):
    v = rng.standard_normal(shape, dtype=np.float32) * np.exp2(rng.integers(-12, 13, shape)).astype(np.float32)
    if cols: v *= np.repeat(np.exp2(rng.integers(-cols, cols + 1, shape[:-2] + (1, shape[-1] // 4))) * (rng.random(shape[:-2] + (1, shape[-1] // 4)) > 0.0625), 4, axis=-1).astype(np.float32)
    return mx_ref.flush(v.astype(BF))
T, CAPP, NB, KK = 1024, 96, 2, 512
MASK = np.repeat(np.arange(128)[:, None] // 16 == np.arange(128)[None] // 16, 4, axis=1)
def lists(rng, agree=False, one=False, full=False, repeat=False):
    a, o = [], []
    for r in range(N):
        n = rng.integers(0, CAPP + 1, (8, N))
        far, most, none = -1, -1, -1
        if one:
            far = (r + rng.integers(1, N)) % N; most, none = rng.permutation(8)[:2]
            n[most, far] = CAPP; n[none, far] = 0
        if full: n[:] = CAPP
        n[n.sum(axis=1) == 0, r] = 1
        e = np.full((8, N, CAPP), -1)
        for g in range(8):
            for q in range(N):
                v = rng.integers(0, T, n[g, q])
                if one and g == most and q == far: v = rng.permutation(T)[:CAPP]
                if full: v[0] = 0; v[1] = T - 1
                e[g, q, rng.permutation(CAPP)[:n[g, q]]] = v
        if agree: e = np.stack([e[0]] * 8)
        e = e.reshape(8, -1); used = [np.flatnonzero(e[g] >= 0) for g in range(8)]
        k = np.stack([np.full(KK, rng.choice(u)) if repeat else rng.choice(u, KK) for u in used])
        if one: k[most, rng.permutation(KK)[:CAPP]] = far * CAPP + rng.permutation(CAPP)
        if full: k[:, 0] = 0; k[:, -1] = N * CAPP - 1
        a.append(gtable(e)); o.append(gtable(k))
    return {"rq": np.stack(a), "od": np.stack(o)}
def setup_inputs(rng):
    ky = f(rng, N, 128, 4 * T); qd = np.array(f(rng, N, 128, NB * 512))
    qd[:, ~np.concatenate([MASK] * NB, axis=1)] = 0
    return {"ky": ky, "qd": qd, **lists(rng)}
def setup_inputs_agree(rng):
    return {**setup_inputs(rng), **lists(rng, agree=True)}
def setup_inputs_one(rng):
    return {**setup_inputs(rng), **lists(rng, one=True)}
def setup_inputs_full(rng):
    return {**setup_inputs(rng), **lists(rng, full=True)}
def setup_inputs_repeat(rng):
    return {**setup_inputs(rng), **lists(rng, repeat=True)}
def setup_inputs_spread(rng):
    d = setup_inputs(rng); d["ky"] = wide(rng, N, 128, 4 * T, cols=8); return d
def check_inputs(d):
    b = []
    for r in range(N):
        e, o = gentries(d["rq"][r]), gentries(d["od"][r])
        if e.min() < -1 or e.max() >= T: b.append("rq")
        if o.min() < 0 or o.max() >= N * CAPP or (np.take_along_axis(e, np.clip(o, 0, N * CAPP - 1), axis=1) < 0).any(): b.append("od")
        if not (d["qd"][r][~np.concatenate([MASK] * NB, axis=1)].astype(np.float32) == 0).all(): b.append("qd")
    return b
def reference(ky, qd, rq, od):
    y = np.zeros((N, 128, NB * KK), np.float32)
    for r in range(N):
        e, o = gentries(rq[r]), gentries(od[r])
        slots = mx_ref.quantize(np.concatenate([gcols(ky[q], e[:, q * CAPP:(q + 1) * CAPP]) for q in range(N)], axis=1))
        for b in range(NB):
            z = mx_ref.matmul(mx_ref.quantize(np.ascontiguousarray(qd[r][:, 512 * b:512 * b + 512])), slots)
            y[r][:, KK * b:KK * b + KK] = gpick(z, o)
    return {"y": y}

@@ -1,0 +1,276 @@
+from concourse.bass import DstId, RemoteDMATransfer
+from concourse.mybir import AluOpType, ActivationFunctionType, dt
+
+N, CAPP, TK, NB, KK = 8, 96, 1024, 2, 512
+LW = CAPP // 16
+COPY = ActivationFunctionType.Copy
+U8 = dt.uint8
+NF, NN = 4, 3
+PAIR = 2 * CAPP
+PAD = 128 - CAPP
+PADC = (N - 1) * CAPP
+OWN = PADC + PAD
+COLS = OWN + CAPP + PAD
+
+TILE = ["f0", "f2", "f1", "f3", "n0", "n1", "n2"]
+CHUNKS = ((0, 192, 64), (192, 192, 64), (384, 192, 64), (576, 128, 0))
+STAGES = {0: (0, 4, "la"), 2: (4, 6, "lb"), 3: (6, 7, "lh")}
+LISTS = [[("f0", "f0.2"), ("f1", "f2.2"), ("f2", "f4.2"), ("f3", "f6.2")],
+         [("n0", "n0.2"), ("n1", "n2.2"), ("n2", "n4.4")]]
+CALLS = [(0, [("hc", 0, "n0.8"), ("fc", 2, "f0.8")]), (0, [("hp", 0, "n0.8"), ("fp", 2, "f0.8")]),
+         (1, [("hc", 1, "n0.8"), ("fc", 3, "f0.8")]), (1, [("fp", 1, "f0.4"), ("fp", 3, "f4.4")]),
+         (2, [("nc", 0, "n0.4"), ("nc", 1, "n4.4")]), (2, [("np", 0, "n0.4"), ("np", 1, "n4.4")]),
+         (3, [("nc", 2, "n0.8")]), (3, [("np", 2, "n0.8")])]
+HELP = [("hc0", [("fc", 0, "f0.8")]), ("hp0", [("fp", 0, "f0.8")]), ("hc1", [("fc", 1, "f0.8")])]
+PRODUCTS = "nmba"
+PIECES = ((0, 160), (160, KK))
+
+SCRATCH = {
+    "rqsb": ("sbuf", [128, N * LW], "int32"),
+    "lst": ("sbuf", [128, (N - 1) * LW], "int32"),
+    "kysb": ("sbuf", [128, 4 * TK], "bfloat16"),
+    "qdsb": ("sbuf", [128, NB * 512], "bfloat16"),
+    "odsb": ("sbuf", [128, KK // 16], "int32"),
+    "odof": ("sbuf", [128, KK // 16], "uint16"),
+    "tile": ("sbuf", [128, 4 * COLS], "bfloat16"),
+    "qc": ("sbuf", [128, PADC + PAD], "float8_e4m3fn_x4"),
+    "qp": ("sbuf", [128, PADC + PAD], "uint8"),
+    "dc": ("sbuf", [128, NB * 128], "float8_e4m3fn_x4"),
+    "dp": ("sbuf", [128, NB * 128], "uint8"),
+    "onc": ("sbuf", [128, 2 * PAIR + PAD], "float8_e4m3fn_x4"),
+    "onp": ("sbuf", [128, 2 * PAIR + PAD], "uint8"),
+    "ofc": ("sbuf", [128, NF * CAPP], "float8_e4m3fn_x4"),
+    "ofp": ("sbuf", [128, NF * CAPP], "uint8"),
+    "hlst": ("sbuf", [128, LW], "int32"),
+    "hcd": ("sbuf", [128, PAIR], "float8_e4m3fn_x4"),
+    "hpl": ("sbuf", [128, PAIR], "uint8"),
+    "z0": ("sbuf", [128, N * CAPP], "float32"),
+    "z1": ("sbuf", [128, N * CAPP], "float32"),
+    "y0": ("sbuf", [128, KK], "float32"),
+    "y1": ("sbuf", [128, KK], "float32"),
+    "ps": ("psum", [128, 512 * 8], "float32"),
+}
+for _t in range(4):
+    SCRATCH["off%d" % _t] = ("sbuf", [128, N * LW], "uint16")
+
+SEMAPHORES = (["ld_rq", "ld_ky", "ld_qd", "ld_od", "la", "lb", "lh", "hl", "hc0", "hc1", "hp0", "sent",
+               "arr_n", "arr_m", "arr_a", "arr_b", "qd_q", "odv", "pad", "q_own", "v_own", "s_own"]
+              + ["%s%d" % (k, t) for k in ("so", "la_", "lb_", "lh_") for t in range(4)]
+              + ["%s%d" % (k, c) for k in ("vg", "sg", "q") for c in range(len(CHUNKS))]
+              + ["mm_%s%d" % (k, b) for k in "nmab" for b in range(NB)]
+              + ["cp0", "cp1"] + ["gy%d%d" % (b, h) for b in range(NB) for h in range(2)] + ["st"])
+
+
+def rank_program(g, core, T, topo):
+    cores, S = T.cores, T.sem
+
+    def on_chip(r):
+        return [q for q in range(N) if topo.chip(cores[q]) == topo.chip(cores[r])]
+
+    def off_chip(r):
+        return [q for q in range(N) if topo.chip(cores[q]) != topo.chip(cores[r])]
+
+    def far_of(r):
+        i, o = on_chip(r).index(r), off_chip(r)
+        return [o[i ^ k] for k in range(NF)]
+
+    def near_of(r):
+        i, o = on_chip(r).index(r), on_chip(r)
+        return [o[i ^ k] for k in (2, 3, 1)]
+
+    def peer(r, name):
+        return (far_of(r) if name[0] == "f" else near_of(r))[int(name[1])]
+
+    def helper_of(r):
+        other = [c for c in topo.cores_of(cores[r]) if topo.die(c) != topo.die(cores[r])]
+        return other[on_chip(r).index(r)]
+
+    rank = T.rank_of(core)
+    mine = [r for r in range(N) if helper_of(r) == core]
+    if rank is None and not mine:
+        return
+    home = mine[0] if rank is None else rank
+    far, near = far_of(home), near_of(home)
+
+    pool = {"f": topo.engines(core, cores[far[0]])}
+    pool["n"] = [e for e in topo.engines(core, cores[near[0]]) if e not in pool["f"]]
+
+    def count(es):
+        return int(es.split(".")[1])
+
+    sent = [0]
+
+    def send(dst, es, sem, src, out):
+        first, n = int(es[1:].split(".")[0]), count(es)
+        rid, pid, _ = topo.addr(dst)
+        sent[0] += n
+        return RemoteDMATransfer(dst_ids=[DstId(rid=rid, pnc=pid)],
+                                 dma_engine_mask=sum(1 << e for e in pool[es[0]][first:first + n]),
+                                 remote_sem=S[sem], srcs=[src], dsts=[out])
+
+    def list_place(r, d):
+        k = LW * [peer(d, x) for x in TILE].index(r)
+        return T.lst[:, k:k + LW]
+
+    def own_place(d):
+        return (OWN, PAIR + CAPP) if near_of(d)[2] < d else (PADC, PAIR)
+
+    def place(kind, r, d):
+        if kind[0] == "f":
+            k = CAPP * off_chip(d).index(r)
+        elif r == near_of(d)[2]:
+            k = PAIR if r < d else PAIR + PAD + CAPP
+        else:
+            k = CAPP * sorted(near_of(d)[:2]).index(r)
+        return T["o" + kind][:, k:k + CAPP]
+
+    def u8(kind, ap):
+        return ap.bitcast(U8) if kind[1] == "c" else ap
+
+    def arrival(kind, k):
+        if kind[0] == "h":
+            return "%s%d" % (kind, k)
+        return "arr_" + (("m" if k == 2 else "n") if kind[0] == "n" else "a" if k < 2 else "b")
+
+    due = {}
+    for _, tr in CALLS + HELP:
+        for kind, k, es in tr:
+            due[arrival(kind, k)] = due.get(arrival(kind, k), 0) + count(es)
+    due["la"] = sum(count(es) for x, es in LISTS[0])
+    due["lb"] = sum(count(es) for x, es in LISTS[1][:2])
+    due["hl"] = count(LISTS[1][2][1])
+    due["lh"] = len(pool["f"])
+
+    if rank is None:
+        d = near[NN - 1]
+        g.wait_ge(S.hl, due["hl"])
+        g.remote_dma_fused([send(cores[d], "f0.%d" % due["lh"], "lh", T.hlst[:], list_place(home, d))], local_sem=S.sent)
+        for sem, tr in HELP:
+            g.wait_ge(S[sem], due[sem])
+            g.remote_dma_fused([send(cores[far[k]], es, arrival(kind, k),
+                                     u8(kind, (T.hcd if kind == "fc" else T.hpl)[:, CAPP * k:CAPP * k + CAPP]),
+                                     u8(kind, place(kind, home, far[k]))) for kind, k, es in tr], local_sem=S.sent)
+        g.wait_ge(S.sent, sent[0])
+        return
+    helper = helper_of(rank)
+
+    g.sync.dma_start(T.rqsb[:], T.rq[:]).then_inc(S.ld_rq, 16)
+    g.sync.dma_start(T.kysb[:], T.ky[:]).then_inc(S.ld_ky, 16)
+    g.sync.wait_ge(S.la, due["la"])
+    g.sync.dma_start(T.qdsb[:], T.qd[:]).then_inc(S.ld_qd, 16)
+    g.sync.dma_start(T.odsb[:], T.od[:]).then_inc(S.ld_od, 16)
+
+    def list_send(x, es, sem):
+        d = peer(rank, x)
+        src = T.rqsb[:, LW * d:LW * d + LW]
+        if x == TILE[-1]:
+            return send(helper, es, "hl", src, T.hlst[:])
+        return send(cores[d], es, sem, src, list_place(rank, d))
+
+    def data_send(kind, k, es):
+        buf = T.qc if kind[1] == "c" else T.qp
+        name = "%s%d" % ("n" if kind[0] == "n" else "f", k)
+        a = CAPP * TILE.index(name)
+        src = u8(kind, buf[:, a:a + CAPP])
+        if kind[0] == "h":
+            out = (T.hcd if kind == "hc" else T.hpl)[:, CAPP * k:CAPP * k + CAPP]
+            return send(helper, es, arrival(kind, k), src, u8(kind, out))
+        d = peer(rank, name)
+        return send(cores[d], es, arrival(kind, k), src, u8(kind, place(kind, rank, d)))
+
+    g.wait_ge(S.ld_rq, 16)
+    for row, sem in zip(LISTS, ("la", "lb")):
+        g.remote_dma_fused([list_send(x, es, sem) for x, es in row], local_sem=S.sent)
+    for c, tr in CALLS:
+        g.wait_ge(S["q%d" % c], 1)
+        g.remote_dma_fused([data_send(*x) for x in tr], local_sem=S.sent)
+    g.wait_ge(S.sent, sent[0])
+
+    V, A = g.vector, g.scalar
+    win = T.kysb[:, 0:4 * TK]
+
+    def offsets(col, src, w, name):
+        for t in range(4):
+            V.tensor_scalar(T["off%d" % t][:, col:col + w], src, 4, t,
+                            AluOpType.mult, AluOpType.add).then_inc(S["%s%d" % (name, t)], 1)
+
+    def gather(q, t, a, col, n, sem):
+        out, src = T.tile[:, 4 * a + t:4 * (a + n):4], win.indirect(T["off%d" % t][:, col:col + n // 16])
+        if q is V:
+            V.tensor_copy(out, src).then_inc(S[sem], 1)
+        else:
+            A.activation(out, src, COPY).then_inc(S[sem], 1)
+
+    for a in (PADC, OWN + CAPP):
+        V.memset(T.tile[:, 4 * a:4 * (a + PAD)], 0.0).then_inc(S.pad, 1)
+    V.wait_ge(S.ld_rq, 16)
+    offsets((N - 1) * LW, T.rqsb[:, LW * rank:LW * rank + LW], LW, "so")
+    V.wait_ge(S.pad, 2)
+    for c, (a, n, s) in enumerate(CHUNKS):
+        if c in STAGES:
+            k0, k1, sem = STAGES[c]
+            V.wait_ge(S[sem], due[sem])
+            offsets(LW * k0, T.lst[:, LW * k0:LW * k1], LW * (k1 - k0), sem + "_")
+        if c == 0:
+            V.wait_ge(S.ld_ky, 16)
+            A.wait_ge(S.ld_ky, 16)
+        m = min(a + n, PADC) - a
+        for q, jobs, done in ((A, [(0, a, m), (1, a, m)] + ([(2, a, s)] if s else []), "sg%d" % c),
+                              (V, [(2, a + s, m - s), (3, a, m)], "vg%d" % c)):
+            for t, b, w in jobs:
+                if c in STAGES:
+                    q.wait_ge(S["%s_%d" % (sem, t)], 1)
+                gather(q, t, b, b // 16, w, done)
+        V.wait_ge(S["vg%d" % c], 2)
+        V.wait_ge(S["sg%d" % c], 3 if s else 2)
+        V.quantize_mx(T.qc[:, a:a + n], T.qp[:, a:a + n], T.tile[:, 4 * a:4 * (a + n)]).then_inc(S["q%d" % c], 1)
+    for q, ts, done in ((A, (0, 1), "s_own"), (V, (2, 3), "v_own")):
+        for t in ts:
+            q.wait_ge(S["so%d" % t], 1)
+            gather(q, t, OWN, (N - 1) * LW, CAPP, done)
+    V.wait_ge(S.s_own, 2)
+    V.wait_ge(S.v_own, 2)
+    a, k = own_place(rank)
+    V.quantize_mx(T.onc[:, k:k + 128], T.onp[:, k:k + 128], T.tile[:, 4 * a:4 * (a + 128)]).then_inc(S.q_own, 1)
+    V.wait_ge(S.ld_qd, 16)
+    V.quantize_mx(T.dc[:], T.dp[:], T.qdsb[:]).then_inc(S.qd_q, 1)
+    V.wait_ge(S.ld_od, 16)
+    V.tensor_copy(T.odof[:], T.odsb[:]).then_inc(S.odv, 1)
+
+    P = g.tensor
+    fa = CAPP * min(off_chip(rank).index(r) for r in far[:2])
+    where = {"n": ("on", 0, CAPP * min(near[:2])),
+             "m": ("on", PAIR + (0 if near[2] < rank else PAD), CAPP * min(near[2], rank)),
+             "a": ("of", fa, CAPP * min(far) + fa), "b": ("of", PAIR - fa, CAPP * min(far) + PAIR - fa)}
+    P.wait_ge(S.qd_q, 1)
+    for j, x in enumerate(PRODUCTS):
+        buf, c0, _ = where[x]
+        P.wait_ge(S["arr_" + x], due["arr_" + x])
+        if x == "m":
+            P.wait_ge(S.q_own, 1)
+        for b in range(NB):
+            o = 512 * (NB * j + b)
+            P.matmul_mx(T.ps[:, o:o + PAIR], T.dc[:, 128 * b:128 * b + 128], T.dp[:, 128 * b:128 * b + 128],
+                        T[buf + "c"][:, c0:c0 + PAIR], T[buf + "p"][:, c0:c0 + PAIR],
+                        True, True).then_inc(S["mm_%s%d" % (x, b)], 1)
+
+    def copies(b, q, put):
+        for j, x in enumerate(PRODUCTS):
+            q.wait_ge(S["mm_%s%d" % (x, b)], 1)
+            o, k = 512 * (NB * j + b), where[x][2]
+            put(T["z%d" % b][:, k:k + PAIR], T.ps[:, o:o + PAIR])
+        q.wait_ge(S["cp%d" % b], len(PRODUCTS))
+        q.wait_ge(S.odv, 1)
+
+    copies(0, V, lambda out, src: V.tensor_copy(out, src).then_inc(S.cp0, 1))
+    copies(1, A, lambda out, src: A.activation(out, src, COPY).then_inc(S.cp1, 1))
+    for h, (k0, k1) in enumerate(PIECES):
+        picks = T.odof[:, k0 // 16:k1 // 16]
+        V.tensor_copy(T.y0[:, k0:k1], T.z0[:].indirect(picks)).then_inc(S["gy0%d" % h], 1)
+        A.activation(T.y1[:, k0:k1], T.z1[:].indirect(picks), COPY).then_inc(S["gy1%d" % h], 1)
+    for h, (k0, k1) in enumerate(PIECES):
+        for b in range(NB):
+            q = A if (b == 1 and h == 1) else g.sync
+            q.wait_ge(S["gy%d%d" % (b, h)], 1)
+            q.dma_start(T.y[:, KK * b + k0:KK * b + k1], T["y%d" % b][:, k0:k1]).then_inc(S.st, 16)
+    g.sync.wait_ge(S.st, 64)

@@ -2,7 +2,9 @@ from concourse.bass import DstId, RemoteDMATransfer
 from concourse.mybir import AluOpType, ActivationFunctionType, dt
 
 N, CAPP, TK, NB, KK = 8, 96, 1024, 2, 512
-LW = CAPP // 16
+NCORES = 64
+RW = CAPP // 16
+LW = 2 * RW
 COPY = ActivationFunctionType.Copy
 U8 = dt.uint8
 NF, NN = 4, 3
@@ -11,27 +13,50 @@ PAD = 128 - CAPP
 PADC = (N - 1) * CAPP
 OWN = PADC + PAD
 COLS = OWN + CAPP + PAD
+SLOTS = N * CAPP
 
 TILE = ["f0", "f2", "f1", "f3", "n0", "n1", "n2"]
-CHUNKS = ((0, 192, 64), (192, 192, 64), (384, 192, 64), (576, 128, 0))
-STAGES = {0: (0, 4, "la"), 2: (4, 6, "lb"), 3: (6, 7, "lh")}
-LISTS = [[("f0", "f0.2"), ("f1", "f2.2"), ("f2", "f4.2"), ("f3", "f6.2")],
+CHUNKS = ((0, 192, 0), (192, 192, 64), (384, 192, 32), (576, 128, 32))
+STAGES = ((0, 2, False), (2, 4, True), (4, 6, True), (6, 7, False))
+OWN_FIRST = False
+OD_AT = (2, 3)
+LISTS = [[("f0", "f0.4"), ("f2", "f4.4")],
+         [("f1", "f0.4"), ("f3", "f4.4")],
          [("n0", "n0.2"), ("n1", "n2.2"), ("n2", "n4.4")]]
-CALLS = [(0, [("hc", 0, "n0.8"), ("fc", 2, "f0.8")]), (0, [("hp", 0, "n0.8"), ("fp", 2, "f0.8")]),
-         (1, [("hc", 1, "n0.8"), ("fc", 3, "f0.8")]), (1, [("fp", 1, "f0.4"), ("fp", 3, "f4.4")]),
-         (2, [("nc", 0, "n0.4"), ("nc", 1, "n4.4")]), (2, [("np", 0, "n0.4"), ("np", 1, "n4.4")]),
-         (3, [("nc", 2, "n0.8")]), (3, [("np", 2, "n0.8")])]
-HELP = [("hc0", [("fc", 0, "f0.8")]), ("hp0", [("fp", 0, "f0.8")]), ("hc1", [("fc", 1, "f0.8")])]
-PRODUCTS = "nmba"
-PIECES = ((0, 160), (160, KK))
+CALLS = [(0, [("c", "f0", "h", "n0.8"), ("c", "f2", "d", "f0.8")]),
+         (0, [("p", "f0", "d", "f0.4"), ("p", "f2", "d", "f4.4")]),
+         (1, [("c", "f1", "h", "n0.8"), ("c", "f3", "d", "f0.8")]),
+         (1, [("p", "f3", "d", "f0.8")]),
+         (1, [("p", "f1", "d", "f0.8")]),
+         (2, [("c", "n0", "d", "n0.4"), ("c", "n1", "d", "n4.4")]),
+         (2, [("p", "n0", "d", "n0.4"), ("p", "n1", "d", "n4.4")]),
+         (3, [("c", "n2", "d", "n0.8")]),
+         (3, [("p", "n2", "d", "n0.8")])]
+MCALLS = [(0, [("c", "f0", "m", "f0.8"), ("c", "f2", "h", "n0.8")]),
+          (0, [("p", "f0", "d", "f0.8"), ("p", "f2", "h", "n0.8")])] + CALLS[2:]
+PRODUCTS = (("n0", "n1"), ("n2", "own"), ("f2", "f3"), ("f0", "f1"))
+PIECES = ((0, 128, 224), (224, 448, 640), (640, 832, NB * KK))
+TILE=["f0","f1","f2","f3","n0","n1","n2"]
+LISTS=[[("f0","f0.4"),("f1","f4.4")],[("f2","f0.4"),("f3","f4.4")],LISTS[2]]
+NEAR=CALLS[5:]
+PRODUCTS=(("n0","n1"),("n2","own"),("f0","f1"),("f2","f3"))
+MPRODUCTS=(("n0","n1"),("n2","own"),("f2","f3"),("f0","f1"))
+CALLS=[(0,[("c","f0","h","n0.8"),("c","f1","d","f0.8")]),(0,[("p","f0+f1","h","n0.8")]),
+(1,[("c","f2","d","f0.4"),("c","f3","d","f4.4")]),(1,[("p","f2+f3","h","n0.8")])]+NEAR
+MCALLS=[(0,[("c","f0","h","n0.8"),("c","f1","m","f0.8")]),(0,[("p","f0","d","f0.4"),("p","f1","d","f4.4")])]+CALLS[2:]
 
 SCRATCH = {
-    "rqsb": ("sbuf", [128, N * LW], "int32"),
-    "lst": ("sbuf", [128, (N - 1) * LW], "int32"),
+    "rqsb": ("sbuf", [128, 2 * N * RW], "int32"),
+    "part": ("sbuf", [128, 2], "int32"),
+    "two": ("sbuf", [128, 1], "float32"),
+    "mine": ("sbuf", [128, N * LW], "uint16"),
+    "lst": ("sbuf", [128, (N - 1) * LW], "uint16"),
+    "odd": ("sbuf", [128, N * LW], "uint16"),
     "kysb": ("sbuf", [128, 4 * TK], "bfloat16"),
     "qdsb": ("sbuf", [128, NB * 512], "bfloat16"),
     "odsb": ("sbuf", [128, KK // 16], "int32"),
-    "odof": ("sbuf", [128, KK // 16], "uint16"),
+    "odw": ("sbuf", [128, 5 * KK // 16], "int32"),
+    "odof": ("sbuf", [128, NB * KK // 16], "uint16"),
     "tile": ("sbuf", [128, 4 * COLS], "bfloat16"),
     "qc": ("sbuf", [128, PADC + PAD], "float8_e4m3fn_x4"),
     "qp": ("sbuf", [128, PADC + PAD], "uint8"),
@@ -41,24 +66,22 @@ SCRATCH = {
     "onp": ("sbuf", [128, 2 * PAIR + PAD], "uint8"),
     "ofc": ("sbuf", [128, NF * CAPP], "float8_e4m3fn_x4"),
     "ofp": ("sbuf", [128, NF * CAPP], "uint8"),
-    "hlst": ("sbuf", [128, LW], "int32"),
-    "hcd": ("sbuf", [128, PAIR], "float8_e4m3fn_x4"),
-    "hpl": ("sbuf", [128, PAIR], "uint8"),
-    "z0": ("sbuf", [128, N * CAPP], "float32"),
-    "z1": ("sbuf", [128, N * CAPP], "float32"),
-    "y0": ("sbuf", [128, KK], "float32"),
-    "y1": ("sbuf", [128, KK], "float32"),
+    "hlst": ("sbuf", [128, LW], "uint16"),
+    "hc": ("sbuf", [128, NF * CAPP], "float8_e4m3fn_x4"),
+    "hp": ("sbuf", [128, NF * CAPP], "uint8"),
+    "z": ("sbuf", [128, NB * SLOTS], "float32"),
+    "ysb": ("sbuf", [128, NB * KK], "float32"),
     "ps": ("psum", [128, 512 * 8], "float32"),
 }
-for _t in range(4):
-    SCRATCH["off%d" % _t] = ("sbuf", [128, N * LW], "uint16")
 
-SEMAPHORES = (["ld_rq", "ld_ky", "ld_qd", "ld_od", "la", "lb", "lh", "hl", "hc0", "hc1", "hp0", "sent",
-               "arr_n", "arr_m", "arr_a", "arr_b", "qd_q", "odv", "pad", "q_own", "v_own", "s_own"]
-              + ["%s%d" % (k, t) for k in ("so", "la_", "lb_", "lh_") for t in range(4)]
+SEMAPHORES = (["ld_rq", "ld_ky", "ld_qd", "ld_od", "hl", "sent", "io", "bit", "two", "mine",
+               "own1", "qd_q", "pad", "q_own", "v_own", "s_own", "cp0", "cp1", "st"]
+              + ["od%d" % k for k in range(4)]
+              + ["%s%d" % (k, j) for k in ("ls", "lp") for j in range(len(STAGES))]
+              + ["arr_" + x for x in TILE] + ["by_%s%s" % (w, x) for w in "cp" for x in TILE[:NF]]
               + ["%s%d" % (k, c) for k in ("vg", "sg", "q") for c in range(len(CHUNKS))]
-              + ["mm_%s%d" % (k, b) for k in "nmab" for b in range(NB)]
-              + ["cp0", "cp1"] + ["gy%d%d" % (b, h) for b in range(NB) for h in range(2)] + ["st"])
+              + ["mm%d%d" % (j, b) for j in range(len(PRODUCTS)) for b in range(NB)]
+              + ["gy%d" % h for h in range(len(PIECES))])
 
 
 def rank_program(g, core, T, topo):
@@ -70,30 +93,41 @@ def rank_program(g, core, T, topo):
     def off_chip(r):
         return [q for q in range(N) if topo.chip(cores[q]) != topo.chip(cores[r])]
 
-    def far_of(r):
-        i, o = on_chip(r).index(r), off_chip(r)
-        return [o[i ^ k] for k in range(NF)]
-
-    def near_of(r):
-        i, o = on_chip(r).index(r), on_chip(r)
-        return [o[i ^ k] for k in (2, 3, 1)]
-
     def peer(r, name):
-        return (far_of(r) if name[0] == "f" else near_of(r))[int(name[1])]
+        if name == "own":
+            return r
+        i, k = on_chip(r).index(r), int(name[1])
+        return off_chip(r)[i ^ k] if name[0] == "f" else on_chip(r)[i ^ (2, 3, 1)[k]]
 
     def helper_of(r):
         other = [c for c in topo.cores_of(cores[r]) if topo.die(c) != topo.die(cores[r])]
         return other[on_chip(r).index(r)]
 
-    rank = T.rank_of(core)
-    mine = [r for r in range(N) if helper_of(r) == core]
-    if rank is None and not mine:
-        return
-    home = mine[0] if rank is None else rank
-    far, near = far_of(home), near_of(home)
+    def mate_of(r):
+        far = cores[off_chip(r)[0]]
+        gates = [c for c in range(NCORES) if topo.mates(topo.chip(c), topo.chip(far)) and topo.may_write(c, far)
+                 and topo.die(c) == topo.die(far)]
+        able = [q for q in on_chip(r) if topo.may_write(cores[q], gates[0])]
+        return gates[able.index(r)] if r in able else None
 
-    pool = {"f": topo.engines(core, cores[far[0]])}
-    pool["n"] = [e for e in topo.engines(core, cores[near[0]]) if e not in pool["f"]]
+    def calls_of(r):
+        return CALLS if mate_of(r) is None else MCALLS
+
+    def items_of(r):
+        return [x for _, tr in calls_of(r) for x in tr]
+
+    rank = T.rank_of(core)
+    served = [(r, road) for r in range(N) for road, c in (("h", helper_of(r)), ("m", mate_of(r))) if c == core
+              and (road == "h" or any(x[2] == road for x in items_of(r)))]
+    if rank is None and not served:
+        return
+    home = served[0][0] if rank is None else rank
+
+    pool = {"f": topo.engines(core, cores[peer(home, "f0")]),
+            "a": topo.engines(core, [c for c in topo.cores_of(core) if c != core][0])}
+    pool["n"] = [e for e in pool["a"] if e not in pool["f"]]
+    pool["e"] = pool["f"][::2]
+    ALL = "f0.%d" % len(pool["f"])
 
     def count(es):
         return int(es.split(".")[1])
@@ -108,169 +142,238 @@ def rank_program(g, core, T, topo):
                                  dma_engine_mask=sum(1 << e for e in pool[es[0]][first:first + n]),
                                  remote_sem=S[sem], srcs=[src], dsts=[out])
 
-    def list_place(r, d):
-        k = LW * [peer(d, x) for x in TILE].index(r)
+    def list_place(name):
+        k = LW * TILE.index(name)
         return T.lst[:, k:k + LW]
 
+    def stage_of(name):
+        return [j for j, (k0, k1, _) in enumerate(STAGES) if name in TILE[k0:k1]][0]
+
     def own_place(d):
-        return (OWN, PAIR + CAPP) if near_of(d)[2] < d else (PADC, PAIR)
+        return (OWN, PAIR + CAPP) if peer(d, "n2") < d else (PADC, PAIR)
 
-    def place(kind, r, d):
-        if kind[0] == "f":
-            k = CAPP * off_chip(d).index(r)
-        elif r == near_of(d)[2]:
-            k = PAIR if r < d else PAIR + PAD + CAPP
-        else:
-            k = CAPP * sorted(near_of(d)[:2]).index(r)
-        return T["o" + kind][:, k:k + CAPP]
+    def landing(r, d):
+        if r in off_chip(d):
+            return "of", CAPP * off_chip(d).index(r)
+        if r == d:
+            return "on", PAIR + (CAPP if peer(d, "n2") < d else PAD)
+        if r == peer(d, "n2"):
+            return "on", PAIR if r < d else PAIR + PAD + CAPP
+        return "on", CAPP * sorted(peer(d, x) for x in ("n0", "n1")).index(r)
 
-    def u8(kind, ap):
-        return ap.bitcast(U8) if kind[1] == "c" else ap
+    def cols(buf, what, k, n=1):
+        ap = T[buf + what][:, k:k + n * CAPP]
+        return ap.bitcast(U8) if what == "c" else ap
 
-    def arrival(kind, k):
-        if kind[0] == "h":
-            return "%s%d" % (kind, k)
-        return "arr_" + (("m" if k == 2 else "n") if kind[0] == "n" else "a" if k < 2 else "b")
+    def share(names, x, road):
+        k = "e" if road == "m" else "f"
+        n = len(pool[k]) // len(names)
+        return "%s%d.%d" % (k, n * names.index(x), n)
 
-    due = {}
-    for _, tr in CALLS + HELP:
-        for kind, k, es in tr:
-            due[arrival(kind, k)] = due.get(arrival(kind, k), 0) + count(es)
-    due["la"] = sum(count(es) for x, es in LISTS[0])
-    due["lb"] = sum(count(es) for x, es in LISTS[1][:2])
-    due["hl"] = count(LISTS[1][2][1])
-    due["lh"] = len(pool["f"])
+    def to_peer(what, name, es, src):
+        d = peer(home, name)
+        buf, k = landing(home, d)
+        return send(cores[d], es, "arr_" + name, src, cols(buf, what, k))
+
+    last = TILE[-1]
+    relayed = dict(x for row in LISTS for x in row)[last]
 
     if rank is None:
-        d = near[NN - 1]
-        g.wait_ge(S.hl, due["hl"])
-        g.remote_dma_fused([send(cores[d], "f0.%d" % due["lh"], "lh", T.hlst[:], list_place(home, d))], local_sem=S.sent)
-        for sem, tr in HELP:
-            g.wait_ge(S[sem], due[sem])
-            g.remote_dma_fused([send(cores[far[k]], es, arrival(kind, k),
-                                     u8(kind, (T.hcd if kind == "fc" else T.hpl)[:, CAPP * k:CAPP * k + CAPP]),
-                                     u8(kind, place(kind, home, far[k]))) for kind, k, es in tr], local_sem=S.sent)
+        if served[0][1] == "h":
+            g.wait_ge(S.hl, count(relayed))
+            g.remote_dma_fused([send(cores[peer(home, last)], ALL, "ls%d" % stage_of(last), T.hlst[:],
+                                     list_place(last))], local_sem=S.sent)
+        for what, name, road, es in items_of(home):
+            if road == served[0][1]:
+                names = name.split("+")
+                g.wait_ge(S["by_" + what + names[0]], count(es))
+                g.remote_dma_fused([to_peer(what, x, share(names, x, road), cols("h", what, CAPP * TILE.index(x)))
+                                    for x in names], local_sem=S.sent)
         g.wait_ge(S.sent, sent[0])
         return
-    helper = helper_of(rank)
+    via = {"h": helper_of(rank), "m": mate_of(rank)}
+    V, A, P = g.vector, g.scalar, g.tensor
+    due = {"arr_" + x: sum(count(es if road == "d" else share(y.split("+"), x, road))
+                           for _, y, road, es in items_of(peer(rank, x)) if x in y.split("+")) for x in TILE}
+    for row in LISTS:
+        for x, es in row:
+            sem = "ls%d" % stage_of(x)
+            due[sem] = due.get(sem, 0) + count(ALL if x == last else es)
 
-    g.sync.dma_start(T.rqsb[:], T.rq[:]).then_inc(S.ld_rq, 16)
+    for s, q in enumerate((g.sync, A)):
+        q.dma_start(T.rqsb[s::2, :], T.rq[:]).then_inc(S.ld_rq, 16)
     g.sync.dma_start(T.kysb[:], T.ky[:]).then_inc(S.ld_ky, 16)
-    g.sync.wait_ge(S.la, due["la"])
+    g.sync.wait_ge(S.ld_ky, 16)
     g.sync.dma_start(T.qdsb[:], T.qd[:]).then_inc(S.ld_qd, 16)
     g.sync.dma_start(T.odsb[:], T.od[:]).then_inc(S.ld_od, 16)
 
-    def list_send(x, es, sem):
+    def list_send(x, es):
         d = peer(rank, x)
-        src = T.rqsb[:, LW * d:LW * d + LW]
-        if x == TILE[-1]:
-            return send(helper, es, "hl", src, T.hlst[:])
-        return send(cores[d], es, sem, src, list_place(rank, d))
+        src = T.mine[:, LW * d:LW * d + LW]
+        if x == last:
+            return send(via["h"], es, "hl", src, T.hlst[:])
+        return send(cores[d], es, "ls%d" % stage_of(x), src, list_place(x))
 
-    def data_send(kind, k, es):
-        buf = T.qc if kind[1] == "c" else T.qp
-        name = "%s%d" % ("n" if kind[0] == "n" else "f", k)
-        a = CAPP * TILE.index(name)
-        src = u8(kind, buf[:, a:a + CAPP])
-        if kind[0] == "h":
-            out = (T.hcd if kind == "hc" else T.hpl)[:, CAPP * k:CAPP * k + CAPP]
-            return send(helper, es, arrival(kind, k), src, u8(kind, out))
-        d = peer(rank, name)
-        return send(cores[d], es, arrival(kind, k), src, u8(kind, place(kind, rank, d)))
+    def data_send(what, name, road, es):
+        names = name.split("+")
+        k = CAPP * TILE.index(names[0])
+        if road == "d":
+            return to_peer(what, name, es, cols("q", what, k))
+        return send(via[road], es, "by_" + what + names[0], cols("q", what, k, len(names)), cols("h", what, k, len(names)))
 
-    g.wait_ge(S.ld_rq, 16)
-    for row, sem in zip(LISTS, ("la", "lb")):
-        g.remote_dma_fused([list_send(x, es, sem) for x, es in row], local_sem=S.sent)
-    for c, tr in CALLS:
+    g.iota(T.part[:, 0:1], [[0, 1]], 0, 1).then_inc(S["io"], 1)
+    g.wait_ge(S.mine, 2)
+    for row in LISTS:
+        g.remote_dma_fused([list_send(x, es) for x, es in row], local_sem=S.sent)
+    for c, tr in calls_of(rank):
         g.wait_ge(S["q%d" % c], 1)
         g.remote_dma_fused([data_send(*x) for x in tr], local_sem=S.sent)
     g.wait_ge(S.sent, sent[0])
 
-    V, A = g.vector, g.scalar
+    Op = AluOpType
+    V.wait_ge(S["io"], 1)
+    V.tensor_scalar(T.part[:, 1:2], T.part[:, 0:1], 1, None, Op.bitwise_and).then_inc(S.bit, 1)
+    V.wait_ge(S.bit, 1)
+    V.tensor_scalar(T.two[:], T.part[:, 1:2], 2, None, Op.mult).then_inc(S.two, 1)
+    for a in (PADC, OWN + CAPP):
+        V.memset(T.tile[:, 4 * a:4 * (a + PAD)], 0.0).then_inc(S.pad, 1)
+    V.wait_ge(S.two, 1)
+    V.wait_ge(S.ld_rq, 32)
+    for h in range(2):
+        V.tensor_scalar(T.mine[:, h::2], T.rqsb[:, N * RW * h:N * RW * (h + 1)], 4, T.two[:],
+                        Op.mult, Op.add).then_inc(S.mine, 1)
+
+    def plus_one(col, src, w, sem):
+        V.tensor_scalar(T.odd[:, col:col + w], src, 1, None, Op.add).then_inc(S[sem], 1)
+
+    V.wait_ge(S.mine, 2)
+    own_even = T.mine[:, LW * rank:LW * rank + LW]
+    plus_one((N - 1) * LW, own_even, LW, "own1")
+    W = KK // 16
+    h, a, h7, d, e = (T.odw[:, W * k:W * k + W] for k in range(5))
+    steps = [0]
+
+    def od_step():
+        k = steps[0]
+        steps[0] += 1
+        if k == 0:
+            V.wait_ge(S.ld_od, 16)
+            V.tensor_scalar(h, T.odsb[:], 1, None, Op.bitwise_and).then_inc(S.od0, 1)
+            V.tensor_scalar(a, T.odsb[:], 1, 7, Op.logical_shift_right, Op.bitwise_and).then_inc(S.od0, 1)
+        elif k == 1:
+            V.wait_ge(S.od0, 2)
+            V.tensor_scalar(h7, h, 7, None, Op.mult).then_inc(S.od1, 1)
+            V.tensor_tensor(d, T.odsb[:], a, Op.subtract).then_inc(S.od1, 1)
+        elif k == 2:
+            V.wait_ge(S.od1, 2)
+            V.tensor_tensor(e, d, h7, Op.add).then_inc(S.od2, 1)
+        elif k == 3:
+            V.wait_ge(S.od2, 1)
+            for b in range(NB):
+                V.tensor_scalar(T.odof[:, W * b:W * b + W], e, SLOTS * b, None, Op.add).then_inc(S.od3, 1)
+
     win = T.kysb[:, 0:4 * TK]
 
-    def offsets(col, src, w, name):
-        for t in range(4):
-            V.tensor_scalar(T["off%d" % t][:, col:col + w], src, 4, t,
-                            AluOpType.mult, AluOpType.add).then_inc(S["%s%d" % (name, t)], 1)
-
-    def gather(q, t, a, col, n, sem):
-        out, src = T.tile[:, 4 * a + t:4 * (a + n):4], win.indirect(T["off%d" % t][:, col:col + n // 16])
+    def gather(q, t, a, n, offsets, sem):
+        out, src = T.tile[:, 4 * a + t:4 * (a + n):2], win.indirect(offsets)
         if q is V:
             V.tensor_copy(out, src).then_inc(S[sem], 1)
         else:
             A.activation(out, src, COPY).then_inc(S[sem], 1)
 
-    for a in (PADC, OWN + CAPP):
-        V.memset(T.tile[:, 4 * a:4 * (a + PAD)], 0.0).then_inc(S.pad, 1)
-    V.wait_ge(S.ld_rq, 16)
-    offsets((N - 1) * LW, T.rqsb[:, LW * rank:LW * rank + LW], LW, "so")
+    def own_gathers():
+        for q in (A, V):
+            q.wait_ge(S.own1, 1)
+        gather(A, 0, OWN, CAPP, own_even, "s_own")
+        gather(V, 1, OWN, CAPP, T.odd[:, (N - 1) * LW:N * LW], "v_own")
+
+    def stages(a0, m):
+        return sorted({stage_of(x) for x in TILE[a0 // CAPP:(a0 + m - 1) // CAPP + 1]})
+
+    made = []
+
+    def lists_plus_one(j):
+        if j not in made:
+            made.append(j)
+            k0, k1, _ = STAGES[j]
+            V.wait_ge(S["ls%d" % j], due["ls%d" % j])
+            plus_one(LW * k0, T.lst[:, LW * k0:LW * k1], LW * (k1 - k0), "lp%d" % j)
+
     V.wait_ge(S.pad, 2)
-    for c, (a, n, s) in enumerate(CHUNKS):
-        if c in STAGES:
-            k0, k1, sem = STAGES[c]
-            V.wait_ge(S[sem], due[sem])
-            offsets(LW * k0, T.lst[:, LW * k0:LW * k1], LW * (k1 - k0), sem + "_")
+    if OWN_FIRST:
+        V.wait_ge(S.ld_ky, 16)
+        A.wait_ge(S.ld_ky, 16)
+        own_gathers()
+    real = [min(a0 + n, PADC) - a0 for a0, n, _ in CHUNKS]
+    for c, (a0, n, s) in enumerate(CHUNKS):
+        m = real[c]
+        for j in stages(a0, m):
+            lists_plus_one(j)
+            A.wait_ge(S["ls%d" % j], due["ls%d" % j])
         if c == 0:
             V.wait_ge(S.ld_ky, 16)
             A.wait_ge(S.ld_ky, 16)
-        m = min(a + n, PADC) - a
-        for q, jobs, done in ((A, [(0, a, m), (1, a, m)] + ([(2, a, s)] if s else []), "sg%d" % c),
-                              (V, [(2, a + s, m - s), (3, a, m)], "vg%d" % c)):
-            for t, b, w in jobs:
-                if c in STAGES:
-                    q.wait_ge(S["%s_%d" % (sem, t)], 1)
-                gather(q, t, b, b // 16, w, done)
-        V.wait_ge(S["vg%d" % c], 2)
-        V.wait_ge(S["sg%d" % c], 3 if s else 2)
-        V.quantize_mx(T.qc[:, a:a + n], T.qp[:, a:a + n], T.tile[:, 4 * a:4 * (a + n)]).then_inc(S["q%d" % c], 1)
-    for q, ts, done in ((A, (0, 1), "s_own"), (V, (2, 3), "v_own")):
-        for t in ts:
-            q.wait_ge(S["so%d" % t], 1)
-            gather(q, t, OWN, (N - 1) * LW, CAPP, done)
-    V.wait_ge(S.s_own, 2)
-    V.wait_ge(S.v_own, 2)
-    a, k = own_place(rank)
-    V.quantize_mx(T.onc[:, k:k + 128], T.onp[:, k:k + 128], T.tile[:, 4 * a:4 * (a + 128)]).then_inc(S.q_own, 1)
+        gather(A, 0, a0, m, T.lst[:, a0 // 8:(a0 + m) // 8], "sg%d" % c)
+        if s:
+            for j in stages(a0, s):
+                A.wait_ge(S["lp%d" % j], 1)
+            gather(A, 1, a0, s, T.odd[:, a0 // 8:(a0 + s) // 8], "sg%d" % c)
+        for j in stages(a0 + s, m - s):
+            V.wait_ge(S["lp%d" % j], 1)
+        gather(V, 1, a0 + s, m - s, T.odd[:, (a0 + s) // 8:(a0 + m) // 8], "vg%d" % c)
+        if c + 1 < len(CHUNKS):
+            for j in stages(CHUNKS[c + 1][0], real[c + 1]):
+                if STAGES[j][2]:
+                    lists_plus_one(j)
+        if c in OD_AT:
+            od_step()
+        V.wait_ge(S["vg%d" % c], 1)
+        V.wait_ge(S["sg%d" % c], 2 if s else 1)
+        V.quantize_mx(T.qc[:, a0:a0 + n], T.qp[:, a0:a0 + n], T.tile[:, 4 * a0:4 * (a0 + n)]).then_inc(S["q%d" % c], 1)
+    if not OWN_FIRST:
+        own_gathers()
     V.wait_ge(S.ld_qd, 16)
     V.quantize_mx(T.dc[:], T.dp[:], T.qdsb[:]).then_inc(S.qd_q, 1)
-    V.wait_ge(S.ld_od, 16)
-    V.tensor_copy(T.odof[:], T.odsb[:]).then_inc(S.odv, 1)
+    od_step()
+    V.wait_ge(S.s_own, 1)
+    V.wait_ge(S.v_own, 1)
+    a0, k = own_place(rank)
+    V.quantize_mx(T.onc[:, k:k + 128], T.onp[:, k:k + 128], T.tile[:, 4 * a0:4 * (a0 + 128)]).then_inc(S.q_own, 1)
+    while steps[0] < 4:
+        od_step()
 
-    P = g.tensor
-    fa = CAPP * min(off_chip(rank).index(r) for r in far[:2])
-    where = {"n": ("on", 0, CAPP * min(near[:2])),
-             "m": ("on", PAIR + (0 if near[2] < rank else PAD), CAPP * min(near[2], rank)),
-             "a": ("of", fa, CAPP * min(far) + fa), "b": ("of", PAIR - fa, CAPP * min(far) + PAIR - fa)}
     P.wait_ge(S.qd_q, 1)
-    for j, x in enumerate(PRODUCTS):
-        buf, c0, _ = where[x]
-        P.wait_ge(S["arr_" + x], due["arr_" + x])
-        if x == "m":
-            P.wait_ge(S.q_own, 1)
+    products = PRODUCTS if via["m"] is None else MPRODUCTS
+    first = [min(peer(rank, x) for x in pair) for pair in products]
+    for j, pair in enumerate(products):
+        buf, c0 = landing(first[j], rank)
+        for x in pair:
+            if x == "own":
+                P.wait_ge(S.q_own, 1)
+            else:
+                P.wait_ge(S["arr_" + x], due["arr_" + x])
         for b in range(NB):
             o = 512 * (NB * j + b)
             P.matmul_mx(T.ps[:, o:o + PAIR], T.dc[:, 128 * b:128 * b + 128], T.dp[:, 128 * b:128 * b + 128],
                         T[buf + "c"][:, c0:c0 + PAIR], T[buf + "p"][:, c0:c0 + PAIR],
-                        True, True).then_inc(S["mm_%s%d" % (x, b)], 1)
+                        True, True).then_inc(S["mm%d%d" % (j, b)], 1)
 
-    def copies(b, q, put):
-        for j, x in enumerate(PRODUCTS):
-            q.wait_ge(S["mm_%s%d" % (x, b)], 1)
-            o, k = 512 * (NB * j + b), where[x][2]
-            put(T["z%d" % b][:, k:k + PAIR], T.ps[:, o:o + PAIR])
-        q.wait_ge(S["cp%d" % b], len(PRODUCTS))
-        q.wait_ge(S.odv, 1)
+    def move(q, out, src, sem):
+        (V.tensor_copy(out, src) if q is V else A.activation(out, src, COPY)).then_inc(S[sem], 1)
 
-    copies(0, V, lambda out, src: V.tensor_copy(out, src).then_inc(S.cp0, 1))
-    copies(1, A, lambda out, src: A.activation(out, src, COPY).then_inc(S.cp1, 1))
-    for h, (k0, k1) in enumerate(PIECES):
-        picks = T.odof[:, k0 // 16:k1 // 16]
-        V.tensor_copy(T.y0[:, k0:k1], T.z0[:].indirect(picks)).then_inc(S["gy0%d" % h], 1)
-        A.activation(T.y1[:, k0:k1], T.z1[:].indirect(picks), COPY).then_inc(S["gy1%d" % h], 1)
-    for h, (k0, k1) in enumerate(PIECES):
-        for b in range(NB):
-            q = A if (b == 1 and h == 1) else g.sync
-            q.wait_ge(S["gy%d%d" % (b, h)], 1)
-            q.dma_start(T.y[:, KK * b + k0:KK * b + k1], T["y%d" % b][:, k0:k1]).then_inc(S.st, 16)
-    g.sync.wait_ge(S.st, 64)
+    for b, q in enumerate((V, A)):
+        for j in range(len(PRODUCTS)):
+            q.wait_ge(S["mm%d%d" % (j, b)], 1)
+            o, k = 512 * (NB * j + b), SLOTS * b + CAPP * first[j]
+            move(q, T.z[:, k:k + PAIR], T.ps[:, o:o + PAIR], "cp%d" % b)
+        q.wait_ge(S.od3, NB)
+    for h, (k0, k1, k2) in enumerate(PIECES):
+        parts = [x for x in ((V, k0, k1), (A, k1, k2)) if x[1] < x[2]]
+        for q, i, j in parts:
+            blocks = (j - 1) // KK + 1
+            for b in range(blocks):
+                q.wait_ge(S["cp%d" % b], len(PRODUCTS))
+            move(q, T.ysb[:, i:j], T.z[:, 0:SLOTS * blocks].indirect(T.odof[:, i // 16:j // 16]), "gy%d" % h)
+        g.sync.wait_ge(S["gy%d" % h], len(parts))
+        g.sync.dma_start(T.y[:, k0:k2], T.ysb[:, k0:k2]).then_inc(S.st, 16)
+    g.sync.wait_ge(S.st, 16 * len(PIECES))

@@ -7,80 +7,149 @@ RW = CAPP // 16
 LW = 2 * RW
 COPY = ActivationFunctionType.Copy
 U8 = dt.uint8
-NF, NN = 4, 3
-PAIR = 2 * CAPP
 PAD = 128 - CAPP
-PADC = (N - 1) * CAPP
-OWN = PADC + PAD
-COLS = OWN + CAPP + PAD
 SLOTS = N * CAPP
+PEERS = ["f0", "f1", "f2", "f3", "n0", "n1", "n2"]
 
-TILE = ["f0", "f2", "f1", "f3", "n0", "n1", "n2"]
-CHUNKS = ((0, 192, 0), (192, 192, 64), (384, 192, 32), (576, 128, 32))
-STAGES = ((0, 2, False), (2, 4, True), (4, 6, True), (6, 7, False))
-OWN_FIRST = False
-OD_AT = (2, 3)
-LISTS = [[("f0", "f0.4"), ("f2", "f4.4")],
-         [("f1", "f0.4"), ("f3", "f4.4")],
-         [("n0", "n0.2"), ("n1", "n2.2"), ("n2", "n4.4")]]
-CALLS = [(0, [("c", "f0", "h", "n0.8"), ("c", "f2", "d", "f0.8")]),
-         (0, [("p", "f0", "d", "f0.4"), ("p", "f2", "d", "f4.4")]),
-         (1, [("c", "f1", "h", "n0.8"), ("c", "f3", "d", "f0.8")]),
-         (1, [("p", "f3", "d", "f0.8")]),
-         (1, [("p", "f1", "d", "f0.8")]),
-         (2, [("c", "n0", "d", "n0.4"), ("c", "n1", "d", "n4.4")]),
-         (2, [("p", "n0", "d", "n0.4"), ("p", "n1", "d", "n4.4")]),
-         (3, [("c", "n2", "d", "n0.8")]),
-         (3, [("p", "n2", "d", "n0.8")])]
-MCALLS = [(0, [("c", "f0", "m", "f0.8"), ("c", "f2", "h", "n0.8")]),
-          (0, [("p", "f0", "d", "f0.8"), ("p", "f2", "h", "n0.8")])] + CALLS[2:]
-PRODUCTS = (("n0", "n1"), ("n2", "own"), ("f2", "f3"), ("f0", "f1"))
+TILE = [PAD, "f0", "f1", PAD, "f2", "f3", "n0", "n1", "n2", 128, "own", PAD]
+CHUNKS = ((("f0",), -PAD, 16, False), (("f1",), PAD, 32, False), (("f2", "f3"), 0, 48, True),
+          (("n0", "n1"), 0, 32, True), (("n2",), PAD, 32, False))
+OWN_S = 32
+OD_AT = (3, 4)
+LISTS = [[("f0", "f0.8")], [("f1", "f0.8"), ("n2", "n0.8")], [("f2", "f0.4"), ("f3", "f4.4")],
+         [("n0", "n0.4"), ("n1", "n4.4")]]
+GATE = "e"
+LOADS = (("qd", "S", "ld_ky"), ("od", "S", None))
+DIAG = False
+STEPS = None
+NPERM = (2, 3, 1)
+LATER = {"H": 1}
+VECTOR = "+0 ky g0 q0 +1 g1 +2 q1 g2 +3 q2 g3 +4 q3 g4 od q4 +5 g5 od q5 go qd od qo od"
+RELAYED = "n2"
+NEAR = [(3, [("c", "n0", "d", "n0.4"), ("c", "n1", "d", "n4.4")]),
+        (3, [("p", "n0", "d", "n0.4"), ("p", "n1", "d", "n4.4")]),
+        (4, [("c", "n2", "d", "n0.8")]),
+        (4, [("p", "n2", "d", "n0.8")])]
+CALLS = {"P": [(0, [("c", "f0", "h", "a0.16")]),
+               (0, [("p", "f0", "d", "f0.8")]),
+               (1, [("c", "f1", "d", "f0.8")]),
+               (1, [("p", "f1", "h", "n0.8")]),
+               (2, [("c", "f2", "d", "f0.4"), ("c", "f3", "d", "f4.4")]),
+               (2, [("p", "f2+f3", "h", "n0.8")])] + NEAR,
+         "M": [(0, [("c", "f0", "m", "f0.8")]),
+               (1, [("c", "f1", "d", "f0.8", 0, 48), ("c", "f1", "h", "n0.4", 48, 96), ("p", "f0+f1", "h", "n4.4")]),
+               (2, [("c", "f2", "h", "n0.8"), ("c", "f3", "d", "f0.8")]),
+               (2, [("p", "f2", "d", "f0.4"), ("p", "f3", "d", "f4.4")])] + NEAR}
+PRODUCTS = {"P": (("f0", "f1"), ("n0", "n1"), ("n2", "own"), ("f2", "f3")),
+            "M": (("f1",), ("n0", "n1"), ("n2", "own"), ("f2", "f3"), ("f0",))}
 PIECES = ((0, 128, 224), (224, 448, 640), (640, 832, NB * KK))
-TILE=["f0","f1","f2","f3","n0","n1","n2"]
-LISTS=[[("f0","f0.4"),("f1","f4.4")],[("f2","f0.4"),("f3","f4.4")],LISTS[2]]
-NEAR=CALLS[5:]
-PRODUCTS=(("n0","n1"),("n2","own"),("f0","f1"),("f2","f3"))
-MPRODUCTS=(("n0","n1"),("n2","own"),("f2","f3"),("f0","f1"))
-CALLS=[(0,[("c","f0","h","n0.8"),("c","f1","d","f0.8")]),(0,[("p","f0+f1","h","n0.8")]),
-(1,[("c","f2","d","f0.4"),("c","f3","d","f4.4")]),(1,[("p","f2+f3","h","n0.8")])]+NEAR
-MCALLS=[(0,[("c","f0","h","n0.8"),("c","f1","m","f0.8")]),(0,[("p","f0","d","f0.4"),("p","f1","d","f4.4")])]+CALLS[2:]
+
+LATE = [(2, [("c", "f2", "h", "n0.8"), ("c", "f3", "d", "f0.8")]),
+        (2, [("p", "f2", "d", "f0.4"), ("p", "f3", "d", "f4.4")])] + NEAR
+CALLS["M"] = [(0, [("c", "f0", "m", "f0.8")]), (1, [("c", "f1", "m", "f0.8")]), (1, [("p", "f0+f1", "h", "n0.8")])] + LATE
+CALLS["P"] = [(0, [("c", "f0", "h", "a0.16")]), (0, [("p", "f0", "d", "f0.8")]),
+              (1, [("c", "f1", "d", "f0.8")]), (1, [("p", "f1", "d", "f0.8")])] + LATE
+PRODUCTS["M"] = (("n0", "n1"), ("n2", "own"), ("f2", "f3"), ("f0", "f1"))
+GATE = "f"
+TILE = [PAD, "f0", "f1", PAD, PAD, "f2", "f3", PAD, "n0", "n1", "n2", 128, "own", PAD]
+CHUNKS = ((("f0",), -PAD, 16, False), (("f1",), PAD, 32, False), (("f2",), -PAD, 32, True), (("f3",), PAD, 32, True),
+          (("n0", "n1"), 0, 32, True), (("n2",), PAD, 32, False))
+OD_AT = (4, 5)
+NEAR = [(c + 1, t) for c, t in NEAR]
+LISTS = [[("f0", "f0.8")], [("f1", "f0.8"), ("n2", "n0.4")], [("f2", "f0.8")],
+         [("f3", "f0.8"), ("n0", "n0.4"), ("n1", "n4.4")]]
+LATE = [(2, [("c", "f2", "h", "n0.8")]), (2, [("p", "f2", "d", "f0.8")]),
+        (3, [("c", "f3", "d", "f0.8")]), (3, [("p", "f3", "d", "f0.8")])] + NEAR
+TILE = [PAD, "f0", "f1", PAD, PAD, "f2", "f3", "n0", "n1", PAD, "n2", 128, "own", PAD]
+CHUNKS = ((("f0",), -PAD, 16), (("f1",), PAD, 32), (("f2",), -PAD, 32), (("f3", "n0"), 0, 48), (("n1",), PAD, 32),
+          (("n2",), PAD, 32))
+VECTOR = "+0 ky g0 +1 q0 g1 +2 q1 g2 +3 q2 g3 +4 q3 g4 od q4 +5 g5 od q5 go qd od qo od"
+LISTS = [[("f0", "f0.8")], [("f1", "f0.8"), ("n2", "n0.4")], [("f2", "f0.8"), ("n0", "n0.8")],
+         [("f3", "f0.8"), ("n1", "n0.8")]]
+LATE = [(2, [("c", "f2", "h", "n0.8")]), (2, [("p", "f2", "d", "f0.8")]),
+        (3, [("c", "f3", "d", "f0.8"), ("c", "n0", "d", "n0.8")]),
+        (3, [("p", "f3", "d", "f0.8"), ("p", "n0", "d", "n0.8")]),
+        (4, [("c", "n1", "d", "n0.8")]), (4, [("p", "n1", "d", "n0.8")]),
+        (5, [("c", "n2", "d", "n0.8")]), (5, [("p", "n2", "d", "n0.8")])]
+PRODUCTS["M"] = (("n0", "n1"), ("f0", "f1"), ("n2", "own"), ("f2", "f3"))
+DIAG = 32
+LOADS = (("od", "S", "ld_ky"), ("qd", "S", None))
+CHUNKS = ((("f0",), -PAD, 16), (("f1",), PAD, 32), (("f2",), -PAD, 32), (("f3", "n0"), 0, 32), (("n1",), PAD, 32),
+          (("n2",), PAD, 48))
+LISTS = [[("f0", "f0.8")], [("f1", "f0.8"), ("n2", "n0.4")], [("f2", "f0.8")],
+         [("f3", "f0.8"), ("n0", "n0.4"), ("n1", "n4.4")]]
+LATE[2:4] = LATE[3], LATE[2]
+PRODUCTS = {"P": (("f0", "f1"), ("n0", "n1"), ("f3",), ("n2", "own"), ("f2",)),
+            "M": (("n0", "n1"), ("f0",), ("n2", "own"), ("f2", "f3"), ("f1",))}
+PIECES = ((0, 128, 256), (256, 448, 640), (640, 832, NB * KK))
+CALLS["M"] = [(0, [("c", "f0", "m", "f0.8", 0, 48), ("c", "f0", "h", "n0.8", 48, 96)])] + CALLS["M"][1:3] + LATE
+HALVES = {c: (c, [("c", "f%d" % c, "d", "f0.8", 0, 48), ("c", "f%d" % c, "h", "n0.8", 48, 96)]) for c in range(4)}
+VECTOR = "ky g0 +1 q0 g1 +2 q1 g2 +34 q2 g3 g4 q3 +5 q4 g5 od q5 od qd od go od qo od"
+STEPS = dict.fromkeys("PM", "00A 01A 10V 11A 20V 21A 30V 31A 40V 41A")
+LISTS = [[("f0", "f0.8")], [("f1", "f0.8")], [("n2", "n0.4", 1), ("n2", "n4.4", 0)], [("f2", "f0.8")],
+         [("f3", "f0.8"), ("n0", "n0.4"), ("n1", "n4.4")]]
+CHUNKS = ((("f0",), -PAD, 0), (("f1",), PAD, 48), (("f2",), -PAD, 48), (("f3", "n0"), 0, 64), (("n1",), PAD, 0),
+          (("n2",), PAD, 32))
+OWN_S = 64
+TILE = [PAD, "f0", "f1", 2 * PAD, "f2", "f3", "n0", "n1", PAD, "n2", 128, "own", PAD]
+CALLS["P"] = CALLS["P"][:4] + LATE
+CALLS["P"][1:4] = [CALLS["P"][2], (1, [("p", "f0", "d", "f0.4"), ("p", "f1", "d", "f4.4")])]
+CALLS["M"][0] = (0, [("c", "f0", "m", "f0.4", 0, 48), ("c", "f0", "d", "f4.4", 48, 96)])
+CALLS["M"][4] = (2, [("p", "f2", "h", "n0.8")])
+
+AT, ZEROS, COLS = {}, [], 0
+for _x in TILE:
+    if isinstance(_x, int):
+        ZEROS.append((COLS, _x))
+        COLS += _x
+    else:
+        AT[_x] = COLS
+        COLS += CAPP
+SENT = AT["n2"] + 128
+FARC = SENT
+VECTOR = VECTOR if "zz" in VECTOR else "z0 zz qz " + VECTOR
+LOADS = LOADS if "ky" in [x[0] for x in LOADS] else (("ky", "S", None),) + LOADS
+STEPS = STEPS or {k: " ".join("%d0V %d1A" % (j, j) for j in range(len(v))) for k, v in PRODUCTS.items()}
+LAND = SLOTS + PAD + 4 * 128
+NPROD = max(len(v) for v in PRODUCTS.values())
+NBY = 8
 
 SCRATCH = {
-    "rqsb": ("sbuf", [128, 2 * N * RW], "int32"),
+    "rqsb": ("sbuf", [128, 2, N, RW], "int32"),
     "part": ("sbuf", [128, 2], "int32"),
-    "two": ("sbuf", [128, 1], "float32"),
-    "mine": ("sbuf", [128, N * LW], "uint16"),
+    "two": ("sbuf", [128, 2], "float32"),
+    "mine": ("sbuf", [128, N, 2, RW], "uint16"),
+    "both": ("sbuf", [128, 4 * LW], "uint16"),
+    "lst0": ("sbuf", [128, 2 * LW], "uint16"),
     "lst": ("sbuf", [128, (N - 1) * LW], "uint16"),
     "odd": ("sbuf", [128, N * LW], "uint16"),
     "kysb": ("sbuf", [128, 4 * TK], "bfloat16"),
     "qdsb": ("sbuf", [128, NB * 512], "bfloat16"),
     "odsb": ("sbuf", [128, KK // 16], "int32"),
-    "odw": ("sbuf", [128, 5 * KK // 16], "int32"),
+    "odw": ("sbuf", [128, 6 * KK // 16], "int32"),
     "odof": ("sbuf", [128, NB * KK // 16], "uint16"),
     "tile": ("sbuf", [128, 4 * COLS], "bfloat16"),
-    "qc": ("sbuf", [128, PADC + PAD], "float8_e4m3fn_x4"),
-    "qp": ("sbuf", [128, PADC + PAD], "uint8"),
+    "qc": ("sbuf", [128, SENT], "float8_e4m3fn_x4"),
+    "qp": ("sbuf", [128, SENT], "uint8"),
     "dc": ("sbuf", [128, NB * 128], "float8_e4m3fn_x4"),
     "dp": ("sbuf", [128, NB * 128], "uint8"),
-    "onc": ("sbuf", [128, 2 * PAIR + PAD], "float8_e4m3fn_x4"),
-    "onp": ("sbuf", [128, 2 * PAIR + PAD], "uint8"),
-    "ofc": ("sbuf", [128, NF * CAPP], "float8_e4m3fn_x4"),
-    "ofp": ("sbuf", [128, NF * CAPP], "uint8"),
-    "hlst": ("sbuf", [128, LW], "uint16"),
-    "hc": ("sbuf", [128, NF * CAPP], "float8_e4m3fn_x4"),
-    "hp": ("sbuf", [128, NF * CAPP], "uint8"),
+    "oc": ("sbuf", [128, LAND], "float8_e4m3fn_x4"),
+    "op": ("sbuf", [128, LAND], "uint8"),
+    "hlst": ("sbuf", [128, RW], "uint16"),
+    "hc": ("sbuf", [128, FARC], "float8_e4m3fn_x4"),
+    "hp": ("sbuf", [128, FARC], "uint8"),
+    "dly": ("sbuf", [128, 300], "int32"),
     "z": ("sbuf", [128, NB * SLOTS], "float32"),
     "ysb": ("sbuf", [128, NB * KK], "float32"),
     "ps": ("psum", [128, 512 * 8], "float32"),
 }
 
-SEMAPHORES = (["ld_rq", "ld_ky", "ld_qd", "ld_od", "hl", "sent", "io", "bit", "two", "mine",
-               "own1", "qd_q", "pad", "q_own", "v_own", "s_own", "cp0", "cp1", "st"]
-              + ["od%d" % k for k in range(4)]
-              + ["%s%d" % (k, j) for k in ("ls", "lp") for j in range(len(STAGES))]
-              + ["arr_" + x for x in TILE] + ["by_%s%s" % (w, x) for w in "cp" for x in TILE[:NF]]
-              + ["%s%d" % (k, c) for k in ("vg", "sg", "q") for c in range(len(CHUNKS))]
-              + ["mm%d%d" % (j, b) for j in range(len(PRODUCTS)) for b in range(NB)]
+SEMAPHORES = (["ld_rq", "ld_ky", "ld_qd", "ld_od", "hl", "sent", "io", "bit", "two", "mine", "first",
+               "own1", "qd0", "qd_q", "pad", "q_zero", "q_own", "g_own", "st"]
+              + ["od%d" % k for k in range(5)]
+              + ["%s%d" % (k, j) for k in ("ls", "lp", "gt", "q") for j in range(len(CHUNKS))]
+              + ["arr_" + x for x in PEERS] + ["by%d" % k for k in range(NBY)]
+              + ["%s%d%d" % (k, j, b) for k in ("mm", "cp") for j in range(NPROD) for b in range(NB)]
               + ["gy%d" % h for h in range(len(PIECES))])
 
 
@@ -97,31 +166,51 @@ def rank_program(g, core, T, topo):
         if name == "own":
             return r
         i, k = on_chip(r).index(r), int(name[1])
-        return off_chip(r)[i ^ k] if name[0] == "f" else on_chip(r)[i ^ (2, 3, 1)[k]]
+        return off_chip(r)[i ^ k] if name[0] == "f" else on_chip(r)[i ^ NPERM[k]]
+
+    def find_gates(far):
+        return [c for c in range(NCORES) if topo.mates(topo.chip(c), topo.chip(far)) and topo.may_write(c, far)]
+
+    gates = [find_gates(cores[off_chip(r)[0]]) for r in range(N)]
+
+    def kind(r):
+        return "M" if topo.may_write(cores[r], gates[r][0]) else "P"
 
     def helper_of(r):
-        other = [c for c in topo.cores_of(cores[r]) if topo.die(c) != topo.die(cores[r])]
-        return other[on_chip(r).index(r)]
+        other = [c for c in topo.cores_of(cores[r]) if topo.die(c) != topo.die(cores[r])
+                 and topo.may_write(c, gates[r][0]) == (kind(r) == "P")]
+        return other[[q for q in on_chip(r) if kind(q) == kind(r)].index(r)]
 
-    def mate_of(r):
-        far = cores[off_chip(r)[0]]
-        gates = [c for c in range(NCORES) if topo.mates(topo.chip(c), topo.chip(far)) and topo.may_write(c, far)
-                 and topo.die(c) == topo.die(far)]
-        able = [q for q in on_chip(r) if topo.may_write(cores[q], gates[0])]
-        return gates[able.index(r)] if r in able else None
+    def gate_of(r):
+        die = topo.die(cores[r] if kind(r) == "M" else helper_of(r))
+        return [c for c in gates[r] if topo.die(c) == die][[q for q in on_chip(r) if kind(q) == kind(r)].index(r)]
 
-    def calls_of(r):
-        return CALLS if mate_of(r) is None else MCALLS
+    def relay_of(r, item):
+        road = item[2]
+        if road == "m":
+            return gate_of(r)
+        if road == "w":
+            return gate_of(peer(r, "n0"))
+        return helper_of({"h": r, "k": peer(r, "n0"), "H": peer(r, item[1][0])}[road])
 
     def items_of(r):
-        return [x for _, tr in calls_of(r) for x in tr]
+        return [(x[0], x[1].split("+"), x[2], x[3]) + (x[4:] or (0, CAPP)) + (c,)
+                for c, tr in CALLS[kind(r)] for x in tr]
+
+    def jobs(c):
+        out, k = [], {"c": 0, "p": 0}
+        todo = [(x[6] + LATER.get(x[2], 0), j, r, x) for r in range(N) for j, x in enumerate(items_of(r))
+                if x[2] != "d" and relay_of(r, x) == c]
+        for _, _, r, x in sorted(todo, key=lambda t: t[:3]):
+            out.append((r, x, k[x[0]]))
+            k[x[0]] += CAPP * len(x[1])
+        return out
 
     rank = T.rank_of(core)
-    served = [(r, road) for r in range(N) for road, c in (("h", helper_of(r)), ("m", mate_of(r))) if c == core
-              and (road == "h" or any(x[2] == road for x in items_of(r)))]
-    if rank is None and not served:
+    helped = [r for r in range(N) if core == helper_of(r)]
+    if rank is None and not helped and not jobs(core):
         return
-    home = served[0][0] if rank is None else rank
+    home = rank if rank is not None else helped[0] if helped else jobs(core)[0][0]
 
     pool = {"f": topo.engines(core, cores[peer(home, "f0")]),
             "a": topo.engines(core, [c for c in topo.cores_of(core) if c != core][0])}
@@ -142,115 +231,146 @@ def rank_program(g, core, T, topo):
                                  dma_engine_mask=sum(1 << e for e in pool[es[0]][first:first + n]),
                                  remote_sem=S[sem], srcs=[src], dsts=[out])
 
-    def list_place(name):
-        k = LW * TILE.index(name)
-        return T.lst[:, k:k + LW]
+    def list_place(name, half=None):
+        k = LW * PEERS.index(name)
+        return T.lst[:, k:k + LW] if half is None else T.lst[:, k + RW * half:k + RW * half + RW]
 
-    def stage_of(name):
-        return [j for j, (k0, k1, _) in enumerate(STAGES) if name in TILE[k0:k1]][0]
+    def chunk_of(name):
+        return [c for c, ch in enumerate(CHUNKS) if name in ch[0]][0]
 
-    def own_place(d):
-        return (OWN, PAIR + CAPP) if peer(d, "n2") < d else (PADC, PAIR)
+    def layout(d):
+        at, spans, zeros, k, shared = {}, [], [], 0, None
+        for pr in PRODUCTS[kind(d)]:
+            names = sorted(pr, key=lambda x: peer(d, x))
+            if len(names) == 1 and names != ["own"]:
+                if shared is None:
+                    shared = k + CAPP
+                    at[names[0]] = k
+                    spans.append((k, 128))
+                    zeros.append(shared)
+                    k += 2 * CAPP + 128
+                else:
+                    at[names[0]] = shared + 128
+                    spans.append((shared + CAPP, 128))
+                    shared = None
+                continue
+            k += PAD if names[-1] != names[0] == "own" else 0
+            spans.append((k, max(128, CAPP * len(names))))
+            for x in names:
+                at[x] = k
+                k += CAPP
+            k += PAD if names[-1] == "own" else 0
+        return at, spans, zeros
 
-    def landing(r, d):
-        if r in off_chip(d):
-            return "of", CAPP * off_chip(d).index(r)
-        if r == d:
-            return "on", PAIR + (CAPP if peer(d, "n2") < d else PAD)
-        if r == peer(d, "n2"):
-            return "on", PAIR if r < d else PAIR + PAD + CAPP
-        return "on", CAPP * sorted(peer(d, x) for x in ("n0", "n1")).index(r)
-
-    def cols(buf, what, k, n=1):
-        ap = T[buf + what][:, k:k + n * CAPP]
+    def cols(buf, what, k, n):
+        ap = T[buf + what][:, k:k + n]
         return ap.bitcast(U8) if what == "c" else ap
 
     def share(names, x, road):
-        k = "e" if road == "m" else "f"
+        k = GATE if road in "mw" else "n" if road == "H" else "f"
         n = len(pool[k]) // len(names)
         return "%s%d.%d" % (k, n * names.index(x), n)
 
-    def to_peer(what, name, es, src):
-        d = peer(home, name)
-        buf, k = landing(home, d)
-        return send(cores[d], es, "arr_" + name, src, cols(buf, what, k))
+    def to_peer(r, buf, k, what, name, es, lo, hi):
+        d = peer(r, name)
+        return send(cores[d], es, "arr_" + name, cols(buf, what, k, hi - lo),
+                    cols("o", what, layout(d)[0][name] + lo, hi - lo))
 
-    last = TILE[-1]
-    relayed = dict(x for row in LISTS for x in row)[last]
+    relayed = [x[1] for row in LISTS for x in row if x[::2] == (RELAYED, 1)][0]
 
     if rank is None:
-        if served[0][1] == "h":
+        if helped:
             g.wait_ge(S.hl, count(relayed))
-            g.remote_dma_fused([send(cores[peer(home, last)], ALL, "ls%d" % stage_of(last), T.hlst[:],
-                                     list_place(last))], local_sem=S.sent)
-        for what, name, road, es in items_of(home):
-            if road == served[0][1]:
-                names = name.split("+")
-                g.wait_ge(S["by_" + what + names[0]], count(es))
-                g.remote_dma_fused([to_peer(what, x, share(names, x, road), cols("h", what, CAPP * TILE.index(x)))
-                                    for x in names], local_sem=S.sent)
+            g.remote_dma_fused([send(cores[peer(home, RELAYED)], ALL, "ls%d" % chunk_of(RELAYED), T.hlst[:],
+                                     list_place(RELAYED, 1))], local_sem=S.sent)
+        for j, (r, (what, names, road, es, lo, hi, _), k) in enumerate(jobs(core)):
+            g.wait_ge(S["by%d" % j], count(es))
+            g.remote_dma_fused([to_peer(r, "h", k + CAPP * i, what, x, share(names, x, road), lo, hi)
+                                for i, x in enumerate(names)], local_sem=S.sent)
         g.wait_ge(S.sent, sent[0])
         return
-    via = {"h": helper_of(rank), "m": mate_of(rank)}
     V, A, P = g.vector, g.scalar, g.tensor
-    due = {"arr_" + x: sum(count(es if road == "d" else share(y.split("+"), x, road))
-                           for _, y, road, es in items_of(peer(rank, x)) if x in y.split("+")) for x in TILE}
+    due = {"arr_" + x: sum(count(y[3] if y[2] == "d" else share(y[1], x, y[2]))
+                           for y in items_of(peer(rank, x)) if x in y[1]) for x in PEERS}
     for row in LISTS:
-        for x, es in row:
-            sem = "ls%d" % stage_of(x)
-            due[sem] = due.get(sem, 0) + count(ALL if x == last else es)
+        for x in row:
+            sem = "ls%d" % chunk_of(x[0])
+            due[sem] = due.get(sem, 0) + count(ALL if x[::2] == (RELAYED, 1) else x[1])
 
     for s, q in enumerate((g.sync, A)):
-        q.dma_start(T.rqsb[s::2, :], T.rq[:]).then_inc(S.ld_rq, 16)
-    g.sync.dma_start(T.kysb[:], T.ky[:]).then_inc(S.ld_ky, 16)
-    g.sync.wait_ge(S.ld_ky, 16)
-    g.sync.dma_start(T.qdsb[:], T.qd[:]).then_inc(S.ld_qd, 16)
-    g.sync.dma_start(T.odsb[:], T.od[:]).then_inc(S.ld_od, 16)
+        q.dma_start(T.rqsb[s::2], T.rq[:]).then_inc(S.ld_rq, 16)
+    for name, q, after in LOADS:
+        q = {"S": g.sync, "A": A}[q]
+        if after:
+            q.wait_ge(S[after], due.get(after, 16 if after == "ld_ky" else 1))
+        if name == "qd" and DIAG:
+            q.wait_ge(S.qd0, 1)
+            for p in range(0, 128, DIAG):
+                for k in range(4 * p, 512 * NB, 512):
+                    q.dma_start(T.qdsb[p:p + DIAG, k:k + 4 * DIAG],
+                                T.qd[p:p + DIAG, k:k + 4 * DIAG]).then_inc(S.ld_qd, 16)
+        else:
+            q.dma_start(T[name + "sb"][:], T[name][:]).then_inc(S["ld_" + name], 16)
 
-    def list_send(x, es):
+    def list_send(x, es, half=None):
         d = peer(rank, x)
-        src = T.mine[:, LW * d:LW * d + LW]
-        if x == last:
-            return send(via["h"], es, "hl", src, T.hlst[:])
-        return send(cores[d], es, "ls%d" % stage_of(x), src, list_place(x))
+        if x == PEERS[0]:
+            return send(cores[d], es, "ls0", T.both[:, 0:2 * LW], T.lst0[:])
+        if (x, half) == (RELAYED, 1):
+            return send(helper_of(rank), es, "hl", T.mine[:, d, 1], T.hlst[:])
+        return send(cores[d], es, "ls%d" % chunk_of(x), T.mine[:, d] if half is None else T.mine[:, d, half],
+                    list_place(x, half))
 
-    def data_send(what, name, road, es):
-        names = name.split("+")
-        k = CAPP * TILE.index(names[0])
+    def data_send(item):
+        what, names, road, es, lo, hi, _ = item
+        a, n = AT[names[0]] + lo, CAPP * (len(names) - 1) + hi - lo
         if road == "d":
-            return to_peer(what, name, es, cols("q", what, k))
-        return send(via[road], es, "by_" + what + names[0], cols("q", what, k, len(names)), cols("h", what, k, len(names)))
+            return to_peer(rank, "q", a, what, names[0], es, lo, hi)
+        relay = relay_of(rank, item)
+        j, k = [(j, k) for j, (r, x, k) in enumerate(jobs(relay)) if (r, x) == (rank, item)][0]
+        return send(relay, es, "by%d" % j, cols("q", what, a, n), cols("h", what, k, n))
 
     g.iota(T.part[:, 0:1], [[0, 1]], 0, 1).then_inc(S["io"], 1)
-    g.wait_ge(S.mine, 2)
-    for row in LISTS:
-        g.remote_dma_fused([list_send(x, es) for x, es in row], local_sem=S.sent)
-    for c, tr in calls_of(rank):
+    for k, row in enumerate(LISTS):
+        if k < 2:
+            g.wait_ge((S.first, S.mine)[k], 2)
+        g.remote_dma_fused([list_send(*x) for x in row], local_sem=S.sent)
+    items = items_of(rank)
+    for c, tr in CALLS[kind(rank)]:
         g.wait_ge(S["q%d" % c], 1)
-        g.remote_dma_fused([data_send(*x) for x in tr], local_sem=S.sent)
+        g.remote_dma_fused([data_send(items.pop(0)) for _ in tr], local_sem=S.sent)
     g.wait_ge(S.sent, sent[0])
 
     Op = AluOpType
+    at, spans, zeros = layout(rank)
     V.wait_ge(S["io"], 1)
     V.tensor_scalar(T.part[:, 1:2], T.part[:, 0:1], 1, None, Op.bitwise_and).then_inc(S.bit, 1)
     V.wait_ge(S.bit, 1)
-    V.tensor_scalar(T.two[:], T.part[:, 1:2], 2, None, Op.mult).then_inc(S.two, 1)
-    for a in (PADC, OWN + CAPP):
-        V.memset(T.tile[:, 4 * a:4 * (a + PAD)], 0.0).then_inc(S.pad, 1)
-    V.wait_ge(S.two, 1)
+    for t in range(2):
+        V.tensor_scalar(T.two[:, t:t + 1], T.part[:, 1:2], 2, t, Op.mult, Op.add).then_inc(S.two, 1)
+    V.wait_ge(S.two, 2)
     V.wait_ge(S.ld_rq, 32)
+
+    def offsets(out, src, t, sem):
+        V.tensor_scalar(out, src, 4, T.two[:, t:t + 1], Op.mult, Op.add).then_inc(S[sem], 1)
+
+    for t in range(2):
+        offsets(T.both[:, LW * t:LW * t + LW], T.rqsb[:, :, peer(rank, PEERS[0])], t, "first")
     for h in range(2):
-        V.tensor_scalar(T.mine[:, h::2], T.rqsb[:, N * RW * h:N * RW * (h + 1)], 4, T.two[:],
-                        Op.mult, Op.add).then_inc(S.mine, 1)
+        offsets(T.mine[:, :, h], T.rqsb[:, h], 0, "mine")
+    for t in range(2):
+        offsets(T.both[:, LW * (2 + t):LW * (3 + t)], T.rqsb[:, :, rank], t, "own1")
+    fills = list(ZEROS)
 
     def plus_one(col, src, w, sem):
         V.tensor_scalar(T.odd[:, col:col + w], src, 1, None, Op.add).then_inc(S[sem], 1)
 
-    V.wait_ge(S.mine, 2)
-    own_even = T.mine[:, LW * rank:LW * rank + LW]
-    plus_one((N - 1) * LW, own_even, LW, "own1")
+    def quantise(buf, k, a, n, sem):
+        V.quantize_mx(T[buf + "c"][:, k:k + n], T[buf + "p"][:, k:k + n],
+                      T.tile[:, 4 * a:4 * (a + n)]).then_inc(S[sem], 1)
+
     W = KK // 16
-    h, a, h7, d, e = (T.odw[:, W * k:W * k + W] for k in range(5))
+    w_h, w_q, w_u, w_t, w_d, w_e = (T.odw[:, W * k:W * k + W] for k in range(6))
     steps = [0]
 
     def od_step():
@@ -258,121 +378,142 @@ def rank_program(g, core, T, topo):
         steps[0] += 1
         if k == 0:
             V.wait_ge(S.ld_od, 16)
-            V.tensor_scalar(h, T.odsb[:], 1, None, Op.bitwise_and).then_inc(S.od0, 1)
-            V.tensor_scalar(a, T.odsb[:], 1, 7, Op.logical_shift_right, Op.bitwise_and).then_inc(S.od0, 1)
+            V.tensor_scalar(w_h, T.odsb[:], 1, None, Op.bitwise_and).then_inc(S.od0, 1)
+            V.tensor_scalar(w_q, T.odsb[:], -(CAPP - 1) / 2, 1 / CAPP, Op.add, Op.mult).then_inc(S.od0, 1)
         elif k == 1:
             V.wait_ge(S.od0, 2)
-            V.tensor_scalar(h7, h, 7, None, Op.mult).then_inc(S.od1, 1)
-            V.tensor_tensor(d, T.odsb[:], a, Op.subtract).then_inc(S.od1, 1)
+            V.tensor_tensor(w_t, w_q, w_h, Op.add).then_inc(S.od1, 1)
+            V.tensor_scalar(w_u, T.odsb[:], 1, None, Op.logical_shift_right).then_inc(S.od1, 1)
         elif k == 2:
             V.wait_ge(S.od1, 2)
-            V.tensor_tensor(e, d, h7, Op.add).then_inc(S.od2, 1)
+            V.tensor_scalar(w_d, w_t, CAPP // 2, None, Op.mult).then_inc(S.od2, 1)
         elif k == 3:
             V.wait_ge(S.od2, 1)
+            V.tensor_tensor(w_e, w_d, w_u, Op.add).then_inc(S.od4, 1)
+        elif k == 4:
+            V.wait_ge(S.od4, 1)
             for b in range(NB):
-                V.tensor_scalar(T.odof[:, W * b:W * b + W], e, SLOTS * b, None, Op.add).then_inc(S.od3, 1)
+                V.tensor_scalar(T.odof[:, W * b:W * b + W], w_e, SLOTS * b, None, Op.add).then_inc(S.od3, 1)
 
     win = T.kysb[:, 0:4 * TK]
-
-    def gather(q, t, a, n, offsets, sem):
-        out, src = T.tile[:, 4 * a + t:4 * (a + n):2], win.indirect(offsets)
-        if q is V:
-            V.tensor_copy(out, src).then_inc(S[sem], 1)
-        else:
-            A.activation(out, src, COPY).then_inc(S[sem], 1)
-
-    def own_gathers():
-        for q in (A, V):
-            q.wait_ge(S.own1, 1)
-        gather(A, 0, OWN, CAPP, own_even, "s_own")
-        gather(V, 1, OWN, CAPP, T.odd[:, (N - 1) * LW:N * LW], "v_own")
-
-    def stages(a0, m):
-        return sorted({stage_of(x) for x in TILE[a0 // CAPP:(a0 + m - 1) // CAPP + 1]})
-
-    made = []
-
-    def lists_plus_one(j):
-        if j not in made:
-            made.append(j)
-            k0, k1, _ = STAGES[j]
-            V.wait_ge(S["ls%d" % j], due["ls%d" % j])
-            plus_one(LW * k0, T.lst[:, LW * k0:LW * k1], LW * (k1 - k0), "lp%d" % j)
-
-    V.wait_ge(S.pad, 2)
-    if OWN_FIRST:
-        V.wait_ge(S.ld_ky, 16)
-        A.wait_ge(S.ld_ky, 16)
-        own_gathers()
-    real = [min(a0 + n, PADC) - a0 for a0, n, _ in CHUNKS]
-    for c, (a0, n, s) in enumerate(CHUNKS):
-        m = real[c]
-        for j in stages(a0, m):
-            lists_plus_one(j)
-            A.wait_ge(S["ls%d" % j], due["ls%d" % j])
-        if c == 0:
-            V.wait_ge(S.ld_ky, 16)
-            A.wait_ge(S.ld_ky, 16)
-        gather(A, 0, a0, m, T.lst[:, a0 // 8:(a0 + m) // 8], "sg%d" % c)
-        if s:
-            for j in stages(a0, s):
-                A.wait_ge(S["lp%d" % j], 1)
-            gather(A, 1, a0, s, T.odd[:, a0 // 8:(a0 + s) // 8], "sg%d" % c)
-        for j in stages(a0 + s, m - s):
-            V.wait_ge(S["lp%d" % j], 1)
-        gather(V, 1, a0 + s, m - s, T.odd[:, (a0 + s) // 8:(a0 + m) // 8], "vg%d" % c)
-        if c + 1 < len(CHUNKS):
-            for j in stages(CHUNKS[c + 1][0], real[c + 1]):
-                if STAGES[j][2]:
-                    lists_plus_one(j)
-        if c in OD_AT:
-            od_step()
-        V.wait_ge(S["vg%d" % c], 1)
-        V.wait_ge(S["sg%d" % c], 2 if s else 1)
-        V.quantize_mx(T.qc[:, a0:a0 + n], T.qp[:, a0:a0 + n], T.tile[:, 4 * a0:4 * (a0 + n)]).then_inc(S["q%d" % c], 1)
-    if not OWN_FIRST:
-        own_gathers()
-    V.wait_ge(S.ld_qd, 16)
-    V.quantize_mx(T.dc[:], T.dp[:], T.qdsb[:]).then_inc(S.qd_q, 1)
-    od_step()
-    V.wait_ge(S.s_own, 1)
-    V.wait_ge(S.v_own, 1)
-    a0, k = own_place(rank)
-    V.quantize_mx(T.onc[:, k:k + 128], T.onp[:, k:k + 128], T.tile[:, 4 * a0:4 * (a0 + 128)]).then_inc(S.q_own, 1)
-    while steps[0] < 4:
-        od_step()
-
-    P.wait_ge(S.qd_q, 1)
-    products = PRODUCTS if via["m"] is None else MPRODUCTS
-    first = [min(peer(rank, x) for x in pair) for pair in products]
-    for j, pair in enumerate(products):
-        buf, c0 = landing(first[j], rank)
-        for x in pair:
-            if x == "own":
-                P.wait_ge(S.q_own, 1)
-            else:
-                P.wait_ge(S["arr_" + x], due["arr_" + x])
-        for b in range(NB):
-            o = 512 * (NB * j + b)
-            P.matmul_mx(T.ps[:, o:o + PAIR], T.dc[:, 128 * b:128 * b + 128], T.dp[:, 128 * b:128 * b + 128],
-                        T[buf + "c"][:, c0:c0 + PAIR], T[buf + "p"][:, c0:c0 + PAIR],
-                        True, True).then_inc(S["mm%d%d" % (j, b)], 1)
 
     def move(q, out, src, sem):
         (V.tensor_copy(out, src) if q is V else A.activation(out, src, COPY)).then_inc(S[sem], 1)
 
-    for b, q in enumerate((V, A)):
-        for j in range(len(PRODUCTS)):
-            q.wait_ge(S["mm%d%d" % (j, b)], 1)
-            o, k = 512 * (NB * j + b), SLOTS * b + CAPP * first[j]
-            move(q, T.z[:, k:k + PAIR], T.ps[:, o:o + PAIR], "cp%d" % b)
+    def gather(q, t, a, n, buf, k, sem):
+        move(q, T.tile[:, 4 * a + t:4 * (a + n):2], win.indirect(buf[:, k:k + n // 8]), sem)
+
+    order = VECTOR.split()
+    ready = {c: "lp" + x[1] for x in order if x[0] == "+" for c in x[1:]}
+    ready = {c: (S[x], 1) for c, x in ready.items()}
+    ready.update({"o": (S.own1, 2), "0": (S.ls0, due["ls0"])})
+    odds = {"o": T.both, "0": T.lst0}
+
+    def part(c):
+        if c == "o":
+            return AT["own"], CAPP, OWN_S, T.both, 2 * LW, 3 * LW, "g_own"
+        names, _, s = CHUNKS[int(c)][:3]
+        if c == "0":
+            return AT[names[0]], CAPP, s, T.lst0, 0, LW, "gt0"
+        k = LW * PEERS.index(names[0])
+        return AT[names[0]], CAPP * len(names), s, T.lst, k, k, "gt" + c
+
+    A.wait_ge(S.ld_ky, 16)
+    for c in [x[1] for x in order if x[0] == "g"]:
+        a0, m, s, even, k, j, sem = part(c)
+        if c != "o":
+            A.wait_ge(S["ls" + c], due["ls" + c])
+        else:
+            A.wait_ge(S.own1, 2)
+        gather(A, 0, a0, m, even, k, sem)
+        if s:
+            A.wait_ge(*ready[c])
+            gather(A, 1, a0, s, odds.get(c, T.odd), j, sem)
+    for x in order:
+        c = x[1]
+        if x == "od":
+            od_step()
+        elif x == "z0":
+            if DIAG:
+                V.memset(T.qdsb[:], 0.0).then_inc(S.qd0, 1)
+        elif x in ("z1", "zz"):
+            for a0, n in [fills.pop() for _ in range(1 if x == "z1" else len(fills))]:
+                V.memset(T.tile[:, 4 * a0:4 * (a0 + n)], 0.0).then_inc(S.pad, 1)
+        elif x == "qz":
+            V.wait_ge(S.pad, len(ZEROS))
+            for k in zeros:
+                quantise("o", k, AT["own"] - 128, 128, "q_zero")
+        elif x == "ky":
+            V.wait_ge(S.ld_ky, 16)
+        elif x == "qd":
+            V.wait_ge(S.ld_qd, 16 * (NB * 128 // DIAG if DIAG else 1))
+            V.quantize_mx(T.dc[:], T.dp[:], T.qdsb[:]).then_inc(S.qd_q, 1)
+        elif x[0] == "+":
+            for u in x[1:]:
+                V.wait_ge(S["ls" + u], due["ls" + u])
+            k, w = part(c)[4], sum(part(u)[1] for u in x[1:]) // 8
+            plus_one(k, T.lst[:, k:k + w], w, "lp" + c)
+        elif x[0] == "g":
+            a0, m, s, _, _, j, sem = part(c)
+            V.wait_ge(*ready[c])
+            gather(V, 1, a0 + s, m - s, odds.get(c, T.odd), j + s // 8, sem)
+        else:
+            a0, m, s, _, _, _, sem = part(c)
+            V.wait_ge(S[sem], 3 if s else 2)
+            if c == "o":
+                z = PAD if [k for k, n in spans if k == at["own"] and n > 128] else 0
+                quantise("o", at["own"] - z, a0 - z, 128, "q_own")
+            else:
+                z = CHUNKS[int(c)][1]
+                quantise("q", a0 + min(z, 0), a0 + min(z, 0), m + abs(z), "q" + c)
+
+    products = PRODUCTS[kind(rank)]
+
+    def bank(j, b):
+        return 512 * ((NB * j + b) % 8)
+
+    P.wait_ge(S.qd_q, 1)
+    if zeros:
+        P.wait_ge(S.q_zero, len(zeros))
+
+    def runs(j):
+        out = []
+        for x in sorted(products[j], key=lambda x: peer(rank, x)):
+            o, k = at[x] - spans[j][0], CAPP * peer(rank, x)
+            if out and out[-1][1] + out[-1][2] == k:
+                out[-1][2] += CAPP
+            else:
+                out.append([o, k, CAPP])
+        return out
+
+    for x in STEPS[kind(rank)].split():
+        j, b, q = int(x[0]), int(x[1]), {"V": V, "A": A}[x[2]]
+        c0, n = spans[j]
+        for x in products[j] if b == 0 else ():
+            if x == "own":
+                P.wait_ge(S.q_own, 1)
+            else:
+                P.wait_ge(S["arr_" + x], due["arr_" + x])
+        if j >= 4:
+            P.wait_ge(S["cp%d%d" % (j - 4, b)], len(runs(j - 4)))
+        o = bank(j, b)
+        P.matmul_mx(T.ps[:, o:o + n], T.dc[:, 128 * b:128 * b + 128], T.dp[:, 128 * b:128 * b + 128],
+                    T.oc[:, c0:c0 + n], T.op[:, c0:c0 + n], True, True).then_inc(S["mm%d%d" % (j, b)], 1)
+        q.wait_ge(S["mm%d%d" % (j, b)], 1)
+        for i, k, n in runs(j):
+            move(q, T.z[:, SLOTS * b + k:SLOTS * b + k + n], T.ps[:, o + i:o + i + n], "cp%d%d" % (j, b))
+
+    for q in (V, A):
         q.wait_ge(S.od3, NB)
+    waited = [0, 0]
     for h, (k0, k1, k2) in enumerate(PIECES):
-        parts = [x for x in ((V, k0, k1), (A, k1, k2)) if x[1] < x[2]]
-        for q, i, j in parts:
+        parts = [x for x in ((0, V, k0, k1), (1, A, k1, k2)) if x[2] < x[3]]
+        for w, q, i, j in parts:
             blocks = (j - 1) // KK + 1
-            for b in range(blocks):
-                q.wait_ge(S["cp%d" % b], len(PRODUCTS))
+            for b in range(waited[w], blocks):
+                for u in range(len(products)):
+                    q.wait_ge(S["cp%d%d" % (u, b)], len(runs(u)))
+            waited[w] = max(waited[w], blocks)
             move(q, T.ysb[:, i:j], T.z[:, 0:SLOTS * blocks].indirect(T.odof[:, i // 16:j // 16]), "gy%d" % h)
         g.sync.wait_ge(S["gy%d" % h], len(parts))
         g.sync.dma_start(T.y[:, k0:k2], T.ysb[:, k0:k2]).then_inc(S.st, 16)

from concourse.bass import DstId, RemoteDMATransfer
from concourse.mybir import AluOpType, ActivationFunctionType, dt

N, CAPP, TK, NB, KK = 8, 96, 1024, 2, 512
NCORES = 64
RW = CAPP // 16
LW = 2 * RW
COPY = ActivationFunctionType.Copy
U8 = dt.uint8
PAD = 128 - CAPP
SLOTS = N * CAPP
PEERS = ["f0", "f1", "f2", "f3", "n0", "n1", "n2"]

TILE = [PAD, "f0", "f1", PAD, "f2", "f3", "n0", "n1", "n2", 128, "own", PAD]
CHUNKS = ((("f0",), -PAD, 16, False), (("f1",), PAD, 32, False), (("f2", "f3"), 0, 48, True),
          (("n0", "n1"), 0, 32, True), (("n2",), PAD, 32, False))
OWN_S = 32
OD_AT = (3, 4)
LISTS = [[("f0", "f0.8")], [("f1", "f0.8"), ("n2", "n0.8")], [("f2", "f0.4"), ("f3", "f4.4")],
         [("n0", "n0.4"), ("n1", "n4.4")]]
GATE = "e"
LOADS = (("qd", "S", "ld_ky"), ("od", "S", None))
DIAG = False
STEPS = None
NPERM = (2, 3, 1)
LATER = {"H": 1}
VECTOR = "+0 ky g0 q0 +1 g1 +2 q1 g2 +3 q2 g3 +4 q3 g4 od q4 +5 g5 od q5 go qd od qo od"
RELAYED = "n2"
NEAR = [(3, [("c", "n0", "d", "n0.4"), ("c", "n1", "d", "n4.4")]),
        (3, [("p", "n0", "d", "n0.4"), ("p", "n1", "d", "n4.4")]),
        (4, [("c", "n2", "d", "n0.8")]),
        (4, [("p", "n2", "d", "n0.8")])]
CALLS = {"P": [(0, [("c", "f0", "h", "a0.16")]),
               (0, [("p", "f0", "d", "f0.8")]),
               (1, [("c", "f1", "d", "f0.8")]),
               (1, [("p", "f1", "h", "n0.8")]),
               (2, [("c", "f2", "d", "f0.4"), ("c", "f3", "d", "f4.4")]),
               (2, [("p", "f2+f3", "h", "n0.8")])] + NEAR,
         "M": [(0, [("c", "f0", "m", "f0.8")]),
               (1, [("c", "f1", "d", "f0.8", 0, 48), ("c", "f1", "h", "n0.4", 48, 96), ("p", "f0+f1", "h", "n4.4")]),
               (2, [("c", "f2", "h", "n0.8"), ("c", "f3", "d", "f0.8")]),
               (2, [("p", "f2", "d", "f0.4"), ("p", "f3", "d", "f4.4")])] + NEAR}
PRODUCTS = {"P": (("f0", "f1"), ("n0", "n1"), ("n2", "own"), ("f2", "f3")),
            "M": (("f1",), ("n0", "n1"), ("n2", "own"), ("f2", "f3"), ("f0",))}
PIECES = ((0, 128, 224), (224, 448, 640), (640, 832, NB * KK))

LATE = [(2, [("c", "f2", "h", "n0.8"), ("c", "f3", "d", "f0.8")]),
        (2, [("p", "f2", "d", "f0.4"), ("p", "f3", "d", "f4.4")])] + NEAR
CALLS["M"] = [(0, [("c", "f0", "m", "f0.8")]), (1, [("c", "f1", "m", "f0.8")]), (1, [("p", "f0+f1", "h", "n0.8")])] + LATE
CALLS["P"] = [(0, [("c", "f0", "h", "a0.16")]), (0, [("p", "f0", "d", "f0.8")]),
              (1, [("c", "f1", "d", "f0.8")]), (1, [("p", "f1", "d", "f0.8")])] + LATE
PRODUCTS["M"] = (("n0", "n1"), ("n2", "own"), ("f2", "f3"), ("f0", "f1"))
GATE = "f"
TILE = [PAD, "f0", "f1", PAD, PAD, "f2", "f3", PAD, "n0", "n1", "n2", 128, "own", PAD]
CHUNKS = ((("f0",), -PAD, 16, False), (("f1",), PAD, 32, False), (("f2",), -PAD, 32, True), (("f3",), PAD, 32, True),
          (("n0", "n1"), 0, 32, True), (("n2",), PAD, 32, False))
OD_AT = (4, 5)
NEAR = [(c + 1, t) for c, t in NEAR]
LISTS = [[("f0", "f0.8")], [("f1", "f0.8"), ("n2", "n0.4")], [("f2", "f0.8")],
         [("f3", "f0.8"), ("n0", "n0.4"), ("n1", "n4.4")]]
LATE = [(2, [("c", "f2", "h", "n0.8")]), (2, [("p", "f2", "d", "f0.8")]),
        (3, [("c", "f3", "d", "f0.8")]), (3, [("p", "f3", "d", "f0.8")])] + NEAR
TILE = [PAD, "f0", "f1", PAD, PAD, "f2", "f3", "n0", "n1", PAD, "n2", 128, "own", PAD]
CHUNKS = ((("f0",), -PAD, 16), (("f1",), PAD, 32), (("f2",), -PAD, 32), (("f3", "n0"), 0, 48), (("n1",), PAD, 32),
          (("n2",), PAD, 32))
VECTOR = "+0 ky g0 +1 q0 g1 +2 q1 g2 +3 q2 g3 +4 q3 g4 od q4 +5 g5 od q5 go qd od qo od"
LISTS = [[("f0", "f0.8")], [("f1", "f0.8"), ("n2", "n0.4")], [("f2", "f0.8"), ("n0", "n0.8")],
         [("f3", "f0.8"), ("n1", "n0.8")]]
LATE = [(2, [("c", "f2", "h", "n0.8")]), (2, [("p", "f2", "d", "f0.8")]),
        (3, [("c", "f3", "d", "f0.8"), ("c", "n0", "d", "n0.8")]),
        (3, [("p", "f3", "d", "f0.8"), ("p", "n0", "d", "n0.8")]),
        (4, [("c", "n1", "d", "n0.8")]), (4, [("p", "n1", "d", "n0.8")]),
        (5, [("c", "n2", "d", "n0.8")]), (5, [("p", "n2", "d", "n0.8")])]
PRODUCTS["M"] = (("n0", "n1"), ("f0", "f1"), ("n2", "own"), ("f2", "f3"))
DIAG = 32
LOADS = (("od", "S", "ld_ky"), ("qd", "S", None))
CHUNKS = ((("f0",), -PAD, 16), (("f1",), PAD, 32), (("f2",), -PAD, 32), (("f3", "n0"), 0, 32), (("n1",), PAD, 32),
          (("n2",), PAD, 48))
LISTS = [[("f0", "f0.8")], [("f1", "f0.8"), ("n2", "n0.4")], [("f2", "f0.8")],
         [("f3", "f0.8"), ("n0", "n0.4"), ("n1", "n4.4")]]
LATE[2:4] = LATE[3], LATE[2]
PRODUCTS = {"P": (("f0", "f1"), ("n0", "n1"), ("f3",), ("n2", "own"), ("f2",)),
            "M": (("n0", "n1"), ("f0",), ("n2", "own"), ("f2", "f3"), ("f1",))}
PIECES = ((0, 128, 256), (256, 448, 640), (640, 832, NB * KK))
CALLS["M"] = [(0, [("c", "f0", "m", "f0.8", 0, 48), ("c", "f0", "h", "n0.8", 48, 96)])] + CALLS["M"][1:3] + LATE
HALVES = {c: (c, [("c", "f%d" % c, "d", "f0.8", 0, 48), ("c", "f%d" % c, "h", "n0.8", 48, 96)]) for c in range(4)}
VECTOR = "ky g0 +1 q0 g1 +2 q1 g2 +34 q2 g3 g4 q3 +5 q4 g5 od q5 od qd od go od qo od"
STEPS = dict.fromkeys("PM", "00A 01A 10V 11A 20V 21A 30V 31A 40V 41A")
LISTS = [[("f0", "f0.8")], [("f1", "f0.8")], [("n2", "n0.4", 1), ("n2", "n4.4", 0)], [("f2", "f0.8")],
         [("f3", "f0.8"), ("n0", "n0.4"), ("n1", "n4.4")]]
CHUNKS = ((("f0",), -PAD, 0), (("f1",), PAD, 48), (("f2",), -PAD, 48), (("f3", "n0"), 0, 64), (("n1",), PAD, 0),
          (("n2",), PAD, 32))
OWN_S = 64
TILE = [PAD, "f0", "f1", 2 * PAD, "f2", "f3", "n0", "n1", PAD, "n2", 128, "own", PAD]
CALLS["P"] = CALLS["P"][:4] + LATE
CALLS["P"][1:4] = [CALLS["P"][2], (1, [("p", "f0", "d", "f0.4"), ("p", "f1", "d", "f4.4")])]
CALLS["M"][0] = (0, [("c", "f0", "m", "f0.4", 0, 48), ("c", "f0", "d", "f4.4", 48, 96)])
CALLS["M"][4] = (2, [("p", "f2", "h", "n0.8")])

AT, ZEROS, COLS = {}, [], 0
for _x in TILE:
    if isinstance(_x, int):
        ZEROS.append((COLS, _x))
        COLS += _x
    else:
        AT[_x] = COLS
        COLS += CAPP
SENT = AT["n2"] + 128
FARC = SENT
VECTOR = VECTOR if "zz" in VECTOR else "z0 zz qz " + VECTOR
LOADS = LOADS if "ky" in [x[0] for x in LOADS] else (("ky", "S", None),) + LOADS
STEPS = STEPS or {k: " ".join("%d0V %d1A" % (j, j) for j in range(len(v))) for k, v in PRODUCTS.items()}
LAND = SLOTS + PAD + 4 * 128
NPROD = max(len(v) for v in PRODUCTS.values())
NBY = 8

SCRATCH = {
    "rqsb": ("sbuf", [128, 2, N, RW], "int32"),
    "part": ("sbuf", [128, 2], "int32"),
    "two": ("sbuf", [128, 2], "float32"),
    "mine": ("sbuf", [128, N, 2, RW], "uint16"),
    "both": ("sbuf", [128, 4 * LW], "uint16"),
    "lst0": ("sbuf", [128, 2 * LW], "uint16"),
    "lst": ("sbuf", [128, (N - 1) * LW], "uint16"),
    "odd": ("sbuf", [128, N * LW], "uint16"),
    "kysb": ("sbuf", [128, 4 * TK], "bfloat16"),
    "qdsb": ("sbuf", [128, NB * 512], "bfloat16"),
    "odsb": ("sbuf", [128, KK // 16], "int32"),
    "odw": ("sbuf", [128, 6 * KK // 16], "int32"),
    "odof": ("sbuf", [128, NB * KK // 16], "uint16"),
    "tile": ("sbuf", [128, 4 * COLS], "bfloat16"),
    "qc": ("sbuf", [128, SENT], "float8_e4m3fn_x4"),
    "qp": ("sbuf", [128, SENT], "uint8"),
    "dc": ("sbuf", [128, NB * 128], "float8_e4m3fn_x4"),
    "dp": ("sbuf", [128, NB * 128], "uint8"),
    "oc": ("sbuf", [128, LAND], "float8_e4m3fn_x4"),
    "op": ("sbuf", [128, LAND], "uint8"),
    "hlst": ("sbuf", [128, RW], "uint16"),
    "hc": ("sbuf", [128, FARC], "float8_e4m3fn_x4"),
    "hp": ("sbuf", [128, FARC], "uint8"),
    "dly": ("sbuf", [128, 300], "int32"),
    "z": ("sbuf", [128, NB * SLOTS], "float32"),
    "ysb": ("sbuf", [128, NB * KK], "float32"),
    "ps": ("psum", [128, 512 * 8], "float32"),
}

SEMAPHORES = (["ld_rq", "ld_ky", "ld_qd", "ld_od", "hl", "sent", "io", "bit", "two", "mine", "first",
               "own1", "qd0", "qd_q", "pad", "q_zero", "q_own", "g_own", "st"]
              + ["od%d" % k for k in range(5)]
              + ["%s%d" % (k, j) for k in ("ls", "lp", "gt", "q") for j in range(len(CHUNKS))]
              + ["arr_" + x for x in PEERS] + ["by%d" % k for k in range(NBY)]
              + ["%s%d%d" % (k, j, b) for k in ("mm", "cp") for j in range(NPROD) for b in range(NB)]
              + ["gy%d" % h for h in range(len(PIECES))])


def rank_program(g, core, T, topo):
    cores, S = T.cores, T.sem

    def on_chip(r):
        return [q for q in range(N) if topo.chip(cores[q]) == topo.chip(cores[r])]

    def off_chip(r):
        return [q for q in range(N) if topo.chip(cores[q]) != topo.chip(cores[r])]

    def peer(r, name):
        if name == "own":
            return r
        i, k = on_chip(r).index(r), int(name[1])
        return off_chip(r)[i ^ k] if name[0] == "f" else on_chip(r)[i ^ NPERM[k]]

    def find_gates(far):
        return [c for c in range(NCORES) if topo.mates(topo.chip(c), topo.chip(far)) and topo.may_write(c, far)]

    gates = [find_gates(cores[off_chip(r)[0]]) for r in range(N)]

    def kind(r):
        return "M" if topo.may_write(cores[r], gates[r][0]) else "P"

    def helper_of(r):
        other = [c for c in topo.cores_of(cores[r]) if topo.die(c) != topo.die(cores[r])
                 and topo.may_write(c, gates[r][0]) == (kind(r) == "P")]
        return other[[q for q in on_chip(r) if kind(q) == kind(r)].index(r)]

    def gate_of(r):
        die = topo.die(cores[r] if kind(r) == "M" else helper_of(r))
        return [c for c in gates[r] if topo.die(c) == die][[q for q in on_chip(r) if kind(q) == kind(r)].index(r)]

    def relay_of(r, item):
        road = item[2]
        if road == "m":
            return gate_of(r)
        if road == "w":
            return gate_of(peer(r, "n0"))
        return helper_of({"h": r, "k": peer(r, "n0"), "H": peer(r, item[1][0])}[road])

    def items_of(r):
        return [(x[0], x[1].split("+"), x[2], x[3]) + (x[4:] or (0, CAPP)) + (c,)
                for c, tr in CALLS[kind(r)] for x in tr]

    def jobs(c):
        out, k = [], {"c": 0, "p": 0}
        todo = [(x[6] + LATER.get(x[2], 0), j, r, x) for r in range(N) for j, x in enumerate(items_of(r))
                if x[2] != "d" and relay_of(r, x) == c]
        for _, _, r, x in sorted(todo, key=lambda t: t[:3]):
            out.append((r, x, k[x[0]]))
            k[x[0]] += CAPP * len(x[1])
        return out

    rank = T.rank_of(core)
    helped = [r for r in range(N) if core == helper_of(r)]
    if rank is None and not helped and not jobs(core):
        return
    home = rank if rank is not None else helped[0] if helped else jobs(core)[0][0]

    pool = {"f": topo.engines(core, cores[peer(home, "f0")]),
            "a": topo.engines(core, [c for c in topo.cores_of(core) if c != core][0])}
    pool["n"] = [e for e in pool["a"] if e not in pool["f"]]
    pool["e"] = pool["f"][::2]
    ALL = "f0.%d" % len(pool["f"])

    def count(es):
        return int(es.split(".")[1])

    sent = [0]

    def send(dst, es, sem, src, out):
        first, n = int(es[1:].split(".")[0]), count(es)
        rid, pid, _ = topo.addr(dst)
        sent[0] += n
        return RemoteDMATransfer(dst_ids=[DstId(rid=rid, pnc=pid)],
                                 dma_engine_mask=sum(1 << e for e in pool[es[0]][first:first + n]),
                                 remote_sem=S[sem], srcs=[src], dsts=[out])

    def list_place(name, half=None):
        k = LW * PEERS.index(name)
        return T.lst[:, k:k + LW] if half is None else T.lst[:, k + RW * half:k + RW * half + RW]

    def chunk_of(name):
        return [c for c, ch in enumerate(CHUNKS) if name in ch[0]][0]

    def layout(d):
        at, spans, zeros, k, shared = {}, [], [], 0, None
        for pr in PRODUCTS[kind(d)]:
            names = sorted(pr, key=lambda x: peer(d, x))
            if len(names) == 1 and names != ["own"]:
                if shared is None:
                    shared = k + CAPP
                    at[names[0]] = k
                    spans.append((k, 128))
                    zeros.append(shared)
                    k += 2 * CAPP + 128
                else:
                    at[names[0]] = shared + 128
                    spans.append((shared + CAPP, 128))
                    shared = None
                continue
            k += PAD if names[-1] != names[0] == "own" else 0
            spans.append((k, max(128, CAPP * len(names))))
            for x in names:
                at[x] = k
                k += CAPP
            k += PAD if names[-1] == "own" else 0
        return at, spans, zeros

    def cols(buf, what, k, n):
        ap = T[buf + what][:, k:k + n]
        return ap.bitcast(U8) if what == "c" else ap

    def share(names, x, road):
        k = GATE if road in "mw" else "n" if road == "H" else "f"
        n = len(pool[k]) // len(names)
        return "%s%d.%d" % (k, n * names.index(x), n)

    def to_peer(r, buf, k, what, name, es, lo, hi):
        d = peer(r, name)
        return send(cores[d], es, "arr_" + name, cols(buf, what, k, hi - lo),
                    cols("o", what, layout(d)[0][name] + lo, hi - lo))

    relayed = [x[1] for row in LISTS for x in row if x[::2] == (RELAYED, 1)][0]

    if rank is None:
        if helped:
            g.wait_ge(S.hl, count(relayed))
            g.remote_dma_fused([send(cores[peer(home, RELAYED)], ALL, "ls%d" % chunk_of(RELAYED), T.hlst[:],
                                     list_place(RELAYED, 1))], local_sem=S.sent)
        for j, (r, (what, names, road, es, lo, hi, _), k) in enumerate(jobs(core)):
            g.wait_ge(S["by%d" % j], count(es))
            g.remote_dma_fused([to_peer(r, "h", k + CAPP * i, what, x, share(names, x, road), lo, hi)
                                for i, x in enumerate(names)], local_sem=S.sent)
        g.wait_ge(S.sent, sent[0])
        return
    V, A, P = g.vector, g.scalar, g.tensor
    due = {"arr_" + x: sum(count(y[3] if y[2] == "d" else share(y[1], x, y[2]))
                           for y in items_of(peer(rank, x)) if x in y[1]) for x in PEERS}
    for row in LISTS:
        for x in row:
            sem = "ls%d" % chunk_of(x[0])
            due[sem] = due.get(sem, 0) + count(ALL if x[::2] == (RELAYED, 1) else x[1])

    for s, q in enumerate((g.sync, A)):
        q.dma_start(T.rqsb[s::2], T.rq[:]).then_inc(S.ld_rq, 16)
    for name, q, after in LOADS:
        q = {"S": g.sync, "A": A}[q]
        if after:
            q.wait_ge(S[after], due.get(after, 16 if after == "ld_ky" else 1))
        if name == "qd" and DIAG:
            q.wait_ge(S.qd0, 1)
            for p in range(0, 128, DIAG):
                for k in range(4 * p, 512 * NB, 512):
                    q.dma_start(T.qdsb[p:p + DIAG, k:k + 4 * DIAG],
                                T.qd[p:p + DIAG, k:k + 4 * DIAG]).then_inc(S.ld_qd, 16)
        else:
            q.dma_start(T[name + "sb"][:], T[name][:]).then_inc(S["ld_" + name], 16)

    def list_send(x, es, half=None):
        d = peer(rank, x)
        if x == PEERS[0]:
            return send(cores[d], es, "ls0", T.both[:, 0:2 * LW], T.lst0[:])
        if (x, half) == (RELAYED, 1):
            return send(helper_of(rank), es, "hl", T.mine[:, d, 1], T.hlst[:])
        return send(cores[d], es, "ls%d" % chunk_of(x), T.mine[:, d] if half is None else T.mine[:, d, half],
                    list_place(x, half))

    def data_send(item):
        what, names, road, es, lo, hi, _ = item
        a, n = AT[names[0]] + lo, CAPP * (len(names) - 1) + hi - lo
        if road == "d":
            return to_peer(rank, "q", a, what, names[0], es, lo, hi)
        relay = relay_of(rank, item)
        j, k = [(j, k) for j, (r, x, k) in enumerate(jobs(relay)) if (r, x) == (rank, item)][0]
        return send(relay, es, "by%d" % j, cols("q", what, a, n), cols("h", what, k, n))

    g.iota(T.part[:, 0:1], [[0, 1]], 0, 1).then_inc(S["io"], 1)
    for k, row in enumerate(LISTS):
        if k < 2:
            g.wait_ge((S.first, S.mine)[k], 2)
        g.remote_dma_fused([list_send(*x) for x in row], local_sem=S.sent)
    items = items_of(rank)
    for c, tr in CALLS[kind(rank)]:
        g.wait_ge(S["q%d" % c], 1)
        g.remote_dma_fused([data_send(items.pop(0)) for _ in tr], local_sem=S.sent)
    g.wait_ge(S.sent, sent[0])

    Op = AluOpType
    at, spans, zeros = layout(rank)
    V.wait_ge(S["io"], 1)
    V.tensor_scalar(T.part[:, 1:2], T.part[:, 0:1], 1, None, Op.bitwise_and).then_inc(S.bit, 1)
    V.wait_ge(S.bit, 1)
    for t in range(2):
        V.tensor_scalar(T.two[:, t:t + 1], T.part[:, 1:2], 2, t, Op.mult, Op.add).then_inc(S.two, 1)
    V.wait_ge(S.two, 2)
    V.wait_ge(S.ld_rq, 32)

    def offsets(out, src, t, sem):
        V.tensor_scalar(out, src, 4, T.two[:, t:t + 1], Op.mult, Op.add).then_inc(S[sem], 1)

    for t in range(2):
        offsets(T.both[:, LW * t:LW * t + LW], T.rqsb[:, :, peer(rank, PEERS[0])], t, "first")
    for h in range(2):
        offsets(T.mine[:, :, h], T.rqsb[:, h], 0, "mine")
    for t in range(2):
        offsets(T.both[:, LW * (2 + t):LW * (3 + t)], T.rqsb[:, :, rank], t, "own1")
    fills = list(ZEROS)

    def plus_one(col, src, w, sem):
        V.tensor_scalar(T.odd[:, col:col + w], src, 1, None, Op.add).then_inc(S[sem], 1)

    def quantise(buf, k, a, n, sem):
        V.quantize_mx(T[buf + "c"][:, k:k + n], T[buf + "p"][:, k:k + n],
                      T.tile[:, 4 * a:4 * (a + n)]).then_inc(S[sem], 1)

    W = KK // 16
    w_h, w_q, w_u, w_t, w_d, w_e = (T.odw[:, W * k:W * k + W] for k in range(6))
    steps = [0]

    def od_step():
        k = steps[0]
        steps[0] += 1
        if k == 0:
            V.wait_ge(S.ld_od, 16)
            V.tensor_scalar(w_h, T.odsb[:], 1, None, Op.bitwise_and).then_inc(S.od0, 1)
            V.tensor_scalar(w_q, T.odsb[:], -(CAPP - 1) / 2, 1 / CAPP, Op.add, Op.mult).then_inc(S.od0, 1)
        elif k == 1:
            V.wait_ge(S.od0, 2)
            V.tensor_tensor(w_t, w_q, w_h, Op.add).then_inc(S.od1, 1)
            V.tensor_scalar(w_u, T.odsb[:], 1, None, Op.logical_shift_right).then_inc(S.od1, 1)
        elif k == 2:
            V.wait_ge(S.od1, 2)
            V.tensor_scalar(w_d, w_t, CAPP // 2, None, Op.mult).then_inc(S.od2, 1)
        elif k == 3:
            V.wait_ge(S.od2, 1)
            V.tensor_tensor(w_e, w_d, w_u, Op.add).then_inc(S.od4, 1)
        elif k == 4:
            V.wait_ge(S.od4, 1)
            for b in range(NB):
                V.tensor_scalar(T.odof[:, W * b:W * b + W], w_e, SLOTS * b, None, Op.add).then_inc(S.od3, 1)

    win = T.kysb[:, 0:4 * TK]

    def move(q, out, src, sem):
        (V.tensor_copy(out, src) if q is V else A.activation(out, src, COPY)).then_inc(S[sem], 1)

    def gather(q, t, a, n, buf, k, sem):
        move(q, T.tile[:, 4 * a + t:4 * (a + n):2], win.indirect(buf[:, k:k + n // 8]), sem)

    order = VECTOR.split()
    ready = {c: "lp" + x[1] for x in order if x[0] == "+" for c in x[1:]}
    ready = {c: (S[x], 1) for c, x in ready.items()}
    ready.update({"o": (S.own1, 2), "0": (S.ls0, due["ls0"])})
    odds = {"o": T.both, "0": T.lst0}

    def part(c):
        if c == "o":
            return AT["own"], CAPP, OWN_S, T.both, 2 * LW, 3 * LW, "g_own"
        names, _, s = CHUNKS[int(c)][:3]
        if c == "0":
            return AT[names[0]], CAPP, s, T.lst0, 0, LW, "gt0"
        k = LW * PEERS.index(names[0])
        return AT[names[0]], CAPP * len(names), s, T.lst, k, k, "gt" + c

    A.wait_ge(S.ld_ky, 16)
    for c in [x[1] for x in order if x[0] == "g"]:
        a0, m, s, even, k, j, sem = part(c)
        if c != "o":
            A.wait_ge(S["ls" + c], due["ls" + c])
        else:
            A.wait_ge(S.own1, 2)
        gather(A, 0, a0, m, even, k, sem)
        if s:
            A.wait_ge(*ready[c])
            gather(A, 1, a0, s, odds.get(c, T.odd), j, sem)
    for x in order:
        c = x[1]
        if x == "od":
            od_step()
        elif x == "z0":
            if DIAG:
                V.memset(T.qdsb[:], 0.0).then_inc(S.qd0, 1)
        elif x in ("z1", "zz"):
            for a0, n in [fills.pop() for _ in range(1 if x == "z1" else len(fills))]:
                V.memset(T.tile[:, 4 * a0:4 * (a0 + n)], 0.0).then_inc(S.pad, 1)
        elif x == "qz":
            V.wait_ge(S.pad, len(ZEROS))
            for k in zeros:
                quantise("o", k, AT["own"] - 128, 128, "q_zero")
        elif x == "ky":
            V.wait_ge(S.ld_ky, 16)
        elif x == "qd":
            V.wait_ge(S.ld_qd, 16 * (NB * 128 // DIAG if DIAG else 1))
            V.quantize_mx(T.dc[:], T.dp[:], T.qdsb[:]).then_inc(S.qd_q, 1)
        elif x[0] == "+":
            for u in x[1:]:
                V.wait_ge(S["ls" + u], due["ls" + u])
            k, w = part(c)[4], sum(part(u)[1] for u in x[1:]) // 8
            plus_one(k, T.lst[:, k:k + w], w, "lp" + c)
        elif x[0] == "g":
            a0, m, s, _, _, j, sem = part(c)
            V.wait_ge(*ready[c])
            gather(V, 1, a0 + s, m - s, odds.get(c, T.odd), j + s // 8, sem)
        else:
            a0, m, s, _, _, _, sem = part(c)
            V.wait_ge(S[sem], 3 if s else 2)
            if c == "o":
                z = PAD if [k for k, n in spans if k == at["own"] and n > 128] else 0
                quantise("o", at["own"] - z, a0 - z, 128, "q_own")
            else:
                z = CHUNKS[int(c)][1]
                quantise("q", a0 + min(z, 0), a0 + min(z, 0), m + abs(z), "q" + c)

    products = PRODUCTS[kind(rank)]

    def bank(j, b):
        return 512 * ((NB * j + b) % 8)

    P.wait_ge(S.qd_q, 1)
    if zeros:
        P.wait_ge(S.q_zero, len(zeros))

    def runs(j):
        out = []
        for x in sorted(products[j], key=lambda x: peer(rank, x)):
            o, k = at[x] - spans[j][0], CAPP * peer(rank, x)
            if out and out[-1][1] + out[-1][2] == k:
                out[-1][2] += CAPP
            else:
                out.append([o, k, CAPP])
        return out

    for x in STEPS[kind(rank)].split():
        j, b, q = int(x[0]), int(x[1]), {"V": V, "A": A}[x[2]]
        c0, n = spans[j]
        for x in products[j] if b == 0 else ():
            if x == "own":
                P.wait_ge(S.q_own, 1)
            else:
                P.wait_ge(S["arr_" + x], due["arr_" + x])
        if j >= 4:
            P.wait_ge(S["cp%d%d" % (j - 4, b)], len(runs(j - 4)))
        o = bank(j, b)
        P.matmul_mx(T.ps[:, o:o + n], T.dc[:, 128 * b:128 * b + 128], T.dp[:, 128 * b:128 * b + 128],
                    T.oc[:, c0:c0 + n], T.op[:, c0:c0 + n], True, True).then_inc(S["mm%d%d" % (j, b)], 1)
        q.wait_ge(S["mm%d%d" % (j, b)], 1)
        for i, k, n in runs(j):
            move(q, T.z[:, SLOTS * b + k:SLOTS * b + k + n], T.ps[:, o + i:o + i + n], "cp%d%d" % (j, b))

    for q in (V, A):
        q.wait_ge(S.od3, NB)
    waited = [0, 0]
    for h, (k0, k1, k2) in enumerate(PIECES):
        parts = [x for x in ((0, V, k0, k1), (1, A, k1, k2)) if x[2] < x[3]]
        for w, q, i, j in parts:
            blocks = (j - 1) // KK + 1
            for b in range(waited[w], blocks):
                for u in range(len(products)):
                    q.wait_ge(S["cp%d%d" % (u, b)], len(runs(u)))
            waited[w] = max(waited[w], blocks)
            move(q, T.ysb[:, i:j], T.z[:, 0:SLOTS * blocks].indirect(T.odof[:, i // 16:j // 16]), "gy%d" % h)
        g.sync.wait_ge(S["gy%d" % h], len(parts))
        g.sync.dma_start(T.y[:, k0:k2], T.ysb[:, k0:k2]).then_inc(S.st, 16)
    g.sync.wait_ge(S.st, 16 * len(PIECES))
